import numpy as np
import ml_dtypes


def mxq(x, axis, fmt="e4m3"):
    dtype, down = {"e4m3": (ml_dtypes.float8_e4m3fn, 7), "e5m2": (ml_dtypes.float8_e5m2, 14)}[fmt]
    v = np.moveaxis(np.asarray(x, np.float32).astype(ml_dtypes.bfloat16).astype(np.float64), axis, -1)
    blocks = v.reshape(v.shape[:-1] + (-1, 32))
    amax = np.abs(blocks).max(-1, keepdims=True)
    byte = np.maximum(np.where(amax > 0, np.frexp(amax)[1] - 1 + 127, 0) - down, 1)
    scale = np.exp2(byte - 127.0)
    codes = (blocks / scale).astype(np.float32).astype(dtype).astype(np.float64)
    return np.moveaxis((codes * scale).reshape(v.shape), -1, axis)


WIDE = False


def mx_kscale(k):
    if not WIDE:
        return np.ones(k)
    levels = np.array([10, -10, 5, -5, 0])
    if k % 512:
        return np.exp2(np.random.permutation(np.resize(levels, k // 32))).repeat(32)
    a = np.empty((k // 512, 16))
    for p in range(k // 512):
        a[p, :8] = np.random.permutation(np.resize(levels, 8))
        for g in range(8):
            far = levels[np.abs(levels - a[p, g]) >= 10]
            a[p, g + 8] = far[np.random.randint(len(far))]
    return np.exp2(a.ravel()).repeat(32)


def f64(x):
    return np.asarray(x).astype(np.float64)


def striped(idx):
    return np.tile(np.asarray(idx).reshape(-1, 16).T, (8, 1)).astype(np.uint16)


def unstriped(offs):
    return offs[:16].T.reshape(-1).astype(np.int64)


def striped8(idx):
    return np.asarray(idx).reshape(8, -1, 16).transpose(0, 2, 1).reshape(128, -1).astype(np.uint16)


def unstriped8(offs):
    return offs.reshape(8, 16, -1).transpose(0, 2, 1).reshape(8, -1).astype(np.int64)


def pick8(x, idx, run):
    r = np.arange(len(x))
    return x[r[:, None], idx[r % (8 * run) // run]]


E2M1 = np.array([0.0, 0.5, 1.0, 1.5, 2.0, 3.0, 4.0, 6.0, -0.0, -0.5, -1.0, -1.5, -2.0, -3.0, -4.0, -6.0])


def pack_weight(w, fmt):
    k, n = w.shape
    w = f64(np.asarray(w, np.float32).astype(ml_dtypes.bfloat16)).reshape(k // 32, 32, n)
    amax = np.abs(w).max(1)
    if fmt == "e4m3":
        byte = np.frexp(amax)[1] - 1 + 127 - 7
    else:
        mant, ex = np.frexp(amax / 6.0)
        byte = np.where(mant > 0.5, ex, ex - 1) + 127
    byte = np.clip(np.where(amax > 0, byte, 1), 1, 254)
    scaled = (w * np.exp2(127.0 - byte)[:, None, :]).reshape(k, n).astype(np.float32)
    by_word = np.ascontiguousarray(scaled.reshape(k // 512, 128, 4, n).transpose(0, 1, 3, 2))
    if fmt == "e4m3":
        words = by_word.astype(ml_dtypes.float8_e4m3fn).view(np.uint8)
    else:
        c = by_word.astype(ml_dtypes.float4_e2m1fn).view(np.uint8) & 0xF
        words = (c[..., 0::2] | (c[..., 1::2] << 4)).reshape(k // 512, 128, 2 * n)
    return np.ascontiguousarray(words), np.ascontiguousarray(byte.astype(np.uint8).reshape(k // 512, 16, n))


def unpack_weight(words, scales, fmt):
    g, _, n = scales.shape
    words = np.ascontiguousarray(words).reshape(g, 128, n, -1)
    if fmt == "e4m3":
        vals = words.view(ml_dtypes.float8_e4m3fn).astype(np.float64)
    else:
        nib = np.empty((g, 128, n, 4), np.uint8)
        nib[..., 0::2] = words & 0xF
        nib[..., 1::2] = words >> 4
        vals = E2M1[nib]
    vals = vals * np.repeat(np.exp2(scales.astype(np.float64) - 127.0), 8, axis=1)[..., None]
    return vals.transpose(0, 1, 3, 2).reshape(g * 512, n)


def bf(x):
    return np.asarray(x, np.float32).astype(ml_dtypes.bfloat16)


def planes(Y):
    r, m = Y.shape
    b = f64(bf(Y)).reshape(r // 32, 32, m)
    amax = np.abs(b).max(1)
    byte = np.clip(np.where(amax > 0, np.frexp(amax)[1] - 1 + 127 - 7, 1), 1, 254)
    codes = (b * np.exp2(127.0 - byte)[:, None, :]).reshape(r, m).astype(np.float32).astype(ml_dtypes.float8_e4m3fn).view(np.uint8)
    words = codes.reshape(r // 512, 128, 4, m).transpose(0, 1, 3, 2)
    return np.ascontiguousarray(words), np.ascontiguousarray(byte.astype(np.uint8).reshape(r // 512, 16, m))


K, U, I, T, E, F = 512, 2048, 256, 512, 512, 512


def setup_inputs():
    n = np.random.standard_normal
    idx = np.random.permutation(U)[:I]
    idx2 = np.stack([np.random.permutation(T)[:I] for _ in range(8)])
    fk = mx_kscale(K)
    fe = mx_kscale(E)
    embp = pack_weight(n((K, U)) / fk[:, None], "e4m3")
    return {
        "emb_words": embp[0],
        "emb_scales": embp[1],
        "wv": (n((K, E)) * 1 / np.sqrt(K) * fk[:, None] * fe).astype(np.float32),
        "base": (n((E, T)) * fe[:, None]).astype(np.float32),
        "wo": (n((E, F)) * 1 / np.sqrt(E) / fe[:, None]).astype(np.float32),
        "offs": striped(idx),
        "offs2": striped8(idx2),
    }


def reference(emb_words, emb_scales, wv, base, wo, offs, offs2):
    idx = unstriped(offs)
    idx2 = unstriped8(offs2)
    embu = unpack_weight(emb_words, emb_scales, "e4m3")
    wvq = mxq(f64(wv), 0, "e4m3")
    embidxg = embu[:, idx]
    v = wvq.T @ embidxg
    vf = np.zeros((E, T))
    vf[np.arange(E)[:, None], idx2[np.arange(E) % 512 // 64]] = v
    x = vf + f64(base)
    woq = mxq(f64(wo), 0, "e4m3")
    xq = mxq(x, 0, "e4m3")
    y = woq.T @ xq
    words, scales = planes(y)
    return y, words, scales

@@ -1,0 +1,160 @@
+from contextlib import ExitStack
+
+import concourse.mybir as mybir
+
+K, U, I, T, E, F = 512, 2048, 256, 512, 512, 512
+FLOPS = 2 * K * E * I + 2 * E * F * T
+
+F32 = mybir.dt.float32
+BF16 = mybir.dt.bfloat16
+I32 = mybir.dt.int32
+U32 = mybir.dt.uint32
+U16 = mybir.dt.uint16
+U8 = mybir.dt.uint8
+FP8X4 = mybir.dt.float8_e4m3fn_x4
+ADD = mybir.AluOpType.add
+
+P = 128
+PACK = 4
+CH = 128
+NCH = T // CH
+
+
+def deal(engine_copy, dealt, raw, m0, m1):
+    engine_copy(
+        dealt[:, :, m0:m1, :].rearrange("p s m j -> p m j s"),
+        raw[:, :, PACK * m0 : PACK * m1].rearrange("p j (m s) -> p m j s", s=PACK),
+    )
+
+
+def weave(engine_copy, woven, planes):
+    engine_copy(
+        woven.rearrange("p (c i) j -> p c j i", i=4),
+        planes.rearrange("p j (c i) -> p c j i", i=4),
+    )
+
+
+def tile_attend_headpage_proj_pl_kernel(tc, emb_words, emb_scales, wv, base, wo, offs, offs2, out_0, out_1, out_2):
+    nc = tc.nc
+    with ExitStack() as ctx:
+        sb = ctx.enter_context(tc.tile_pool(name="sb", bufs=1))
+        ps = ctx.enter_context(tc.psum_pool(name="ps", bufs=1))
+
+        offs_sb = sb.tile([P, I // 16], U16, name="offs_sb")
+        offs2_sb = sb.tile([P, I // 16], U16, name="offs2_sb")
+        wv_raw = sb.tile([P, PACK, E], F32, name="wv_raw", align_bytes=64)
+        words = sb.tile([P, U], I32, name="words", tag="words_then_wo", align_bytes=64)
+        scale_rows = sb.tile([P, U], U8, name="scale_rows", tag="rows_then_base", align_bytes=64)
+        emb_scale = sb.tile([P, I], U8, name="emb_scale", align_bytes=64)
+
+        nc.scalar.dma_start(scale_rows[16:32, :].bitcast(I32), emb_scales[0].bitcast(I32))
+        nc.vector.memset(scale_rows[0:16, :].bitcast(I32), 0)
+        nc.gpsimd.memset(scale_rows[32:64, :].bitcast(I32), 0)
+        nc.vector.memset(scale_rows[64:P, :].bitcast(I32), 0)
+        nc.vector.memset(emb_scale[:].bitcast(I32), 0)
+        nc.sync.dma_start(wv_raw[:], wv.rearrange("(p j) e -> p j e", j=PACK))
+        nc.sync.dma_start(offs_sb[:], offs)
+        nc.sync.dma_start(offs2_sb[:], offs2)
+        nc.sync.dma_start(words[:], emb_words[0].rearrange("p u r -> p (u r)").bitcast(I32))
+
+        picked_rows = sb.tile([P, I], U8, name="picked_rows", align_bytes=64)
+        nc.vector.tensor_copy(picked_rows[:], scale_rows[:].indirect(offs_sb[:]))
+        for q in range(4):
+            nc.scalar.dma_start(
+                emb_scale[32 * q : 32 * q + 4, :].bitcast(I32),
+                picked_rows[16 + 4 * q : 20 + 4 * q, :].bitcast(I32),
+            )
+
+        base_sb = sb.tile([P, PACK, T], F32, name="base_sb", tag="rows_then_base", align_bytes=64)
+        nc.sync.dma_start(base_sb[:], base.rearrange("(p j) t -> p j t", j=PACK))
+
+        wv_dealt = sb.tile([P, PACK, P, PACK], BF16, name="wv_dealt", align_bytes=64)
+        deal(nc.scalar.copy, wv_dealt, wv_raw, 0, 40)
+        deal(nc.vector.tensor_copy, wv_dealt, wv_raw, 40, P)
+        wv_codes = sb.tile([P, E], U32, name="wv_codes", align_bytes=64)
+        wv_scale = sb.tile([P, E], U8, name="wv_scale", align_bytes=64)
+        nc.vector.quantize_mx(wv_codes[:].bitcast(FP8X4), wv_scale[:], wv_dealt[:].rearrange("p s m j -> p (s m j)"))
+
+        emb_codes = sb.tile([P, I], U32, name="emb_codes", align_bytes=64)
+        nc.vector.tensor_copy(emb_codes[:], words[:].bitcast(U32).indirect(offs_sb[:]))
+
+        wo_raw = sb.tile([P, PACK, F], F32, name="wo_raw", tag="words_then_wo", align_bytes=64)
+        nc.sync.dma_start(wo_raw[:], wo.rearrange("(p j) f -> p j f", j=PACK))
+
+        pages = [sb.tile([P, T], F32, name="page%d" % j, align_bytes=64) for j in range(PACK)]
+        for j in range(PACK):
+            nc.vector.memset(pages[j][:], 0.0)
+
+        x_planes = sb.tile([P, PACK, T], BF16, name="x_planes", align_bytes=64)
+        for j in range(PACK):
+            cols = slice(P * j, P * (j + 1))
+            v_ps = ps.tile([P, I], F32, name="v_ps%d" % j)
+            nc.tensor.matmul_mx(
+                v_ps[:], lhsT=wv_codes[:, cols].bitcast(FP8X4), lhsT_scale=wv_scale[:, cols],
+                rhs=emb_codes[:].bitcast(FP8X4), rhs_scale=emb_scale[:], start=True, stop=True,
+            )
+            v_sb = sb.tile([P, I], F32, name="v_sb%d" % j, align_bytes=64)
+            nc.scalar.copy(v_sb[:], v_ps[:])
+            nc.vector.tensor_copy(pages[j][:].indirect(offs2_sb[:]), v_sb[:])
+            if j < PACK - 1:
+                nc.gpsimd.tensor_tensor(x_planes[:, j, :], pages[j][:], base_sb[:, j, :], ADD)
+
+        wo_dealt = sb.tile([P, PACK, P, PACK], BF16, name="wo_dealt", align_bytes=64)
+        deal(nc.scalar.copy, wo_dealt, wo_raw, 0, P)
+        wo_codes = sb.tile([P, F], U32, name="wo_codes", align_bytes=64)
+        wo_scale = sb.tile([P, F], U8, name="wo_scale", align_bytes=64)
+        nc.vector.quantize_mx(wo_codes[:].bitcast(FP8X4), wo_scale[:], wo_dealt[:].rearrange("p s m j -> p (s m j)"))
+
+        y_sb = sb.tile([P, PACK, T], F32, name="y_sb", align_bytes=64)
+        y_codes = sb.tile([P, T], U32, name="y_codes", align_bytes=64)
+        y_scale = sb.tile([P, T], U8, name="y_scale", align_bytes=64)
+        y_hbm = out_0.rearrange("(p s) t -> p s t", s=PACK)
+        codes_hbm = out_1[0].rearrange("p t r -> p (t r)").bitcast(I32)
+        x_woven, x_codes, x_scale, y_ps, y_woven = {}, {}, {}, {}, {}
+
+        def cols_of(c):
+            return slice(CH * c, CH * (c + 1))
+
+        def add_last(c):
+            nc.vector.tensor_tensor(x_planes[:, 3, cols_of(c)], pages[3][:, cols_of(c)], base_sb[:, 3, cols_of(c)], ADD)
+
+        def weave_x(c):
+            x_woven[c] = sb.tile([P, CH, PACK], BF16, name="x_woven%d" % c, align_bytes=64)
+            weave(nc.vector.tensor_copy if c % 2 == 0 else nc.scalar.copy, x_woven[c][:], x_planes[:, :, cols_of(c)])
+
+        def project(c):
+            x_codes = sb.tile([P, CH], U32, name="x_codes%d" % c, align_bytes=64)
+            x_scale = sb.tile([P, CH], U8, name="x_scale%d" % c, align_bytes=64)
+            nc.vector.quantize_mx(x_codes[:].bitcast(FP8X4), x_scale[:], x_woven[c][:].rearrange("p t j -> p (t j)"))
+            y_ps = ps.tile([P, PACK, CH], F32, name="y_ps%d" % c)
+            for s in range(PACK):
+                cols = slice(P * s, P * (s + 1))
+                nc.tensor.matmul_mx(
+                    y_ps[:, s, :], lhsT=wo_codes[:, cols].bitcast(FP8X4), lhsT_scale=wo_scale[:, cols],
+                    rhs=x_codes[:].bitcast(FP8X4), rhs_scale=x_scale[:], start=True, stop=True,
+                )
+            nc.scalar.copy(y_sb[:, :, cols_of(c)], y_ps[:])
+            nc.sync.dma_start(y_hbm[:, :, cols_of(c)], y_sb[:, :, cols_of(c)])
+
+        def weave_y(c):
+            y_woven[c] = sb.tile([P, CH, PACK], BF16, name="y_woven%d" % c, align_bytes=64)
+            weave(nc.vector.tensor_copy, y_woven[c][:], y_sb[:, :, cols_of(c)])
+
+        def quantize_y(c):
+            nc.vector.quantize_mx(y_codes[:, cols_of(c)].bitcast(FP8X4), y_scale[:, cols_of(c)], y_woven[c][:].rearrange("p t j -> p (t j)"))
+
+        for c in range(NCH):
+            add_last(c)
+        for c in range(NCH):
+            weave_x(c)
+        for c in range(NCH):
+            project(c)
+        for c in range(NCH):
+            weave_y(c)
+            if c > 0:
+                quantize_y(c - 1)
+        quantize_y(NCH - 1)
+        nc.sync.dma_start(codes_hbm, y_codes[:].bitcast(I32))
+        for q in range(4):
+            queue = nc.scalar if q % 2 else nc.sync
+            queue.dma_start(out_2[0, 4 * q : 4 * q + 4, :].bitcast(I32), y_scale[32 * q : 32 * q + 4, :].bitcast(I32))

@@ -43,43 +43,34 @@ def tile_attend_headpage_proj_pl_kernel(tc, emb_words, emb_scales, wv, base, wo,
         offs_sb = sb.tile([P, I // 16], U16, name="offs_sb")
         offs2_sb = sb.tile([P, I // 16], U16, name="offs2_sb")
         wv_raw = sb.tile([P, PACK, E], F32, name="wv_raw", align_bytes=64)
-        words = sb.tile([P, U], I32, name="words", tag="words_then_wo", align_bytes=64)
-        scale_rows = sb.tile([P, U], U8, name="scale_rows", tag="rows_then_base", align_bytes=64)
-        emb_scale = sb.tile([P, I], U8, name="emb_scale", align_bytes=64)
+        wo_raw = sb.tile([P, PACK, F], F32, name="wo_raw", align_bytes=64)
+        base_sb = sb.tile([P, PACK, T], F32, name="base_sb", align_bytes=64)
+        words = sb.tile([P, U], I32, name="words", align_bytes=64)
+        scale_rows = sb.tile([P, U], U8, name="scale_rows", align_bytes=64)
 
-        nc.scalar.dma_start(scale_rows[16:32, :].bitcast(I32), emb_scales[0].bitcast(I32))
-        nc.vector.memset(scale_rows[0:16, :].bitcast(I32), 0)
-        nc.gpsimd.memset(scale_rows[32:64, :].bitcast(I32), 0)
-        nc.vector.memset(scale_rows[64:P, :].bitcast(I32), 0)
-        nc.vector.memset(emb_scale[:].bitcast(I32), 0)
+        nc.vector.memset(scale_rows[:].bitcast(I32), 0)
         nc.sync.dma_start(wv_raw[:], wv.rearrange("(p j) e -> p j e", j=PACK))
-        nc.sync.dma_start(offs_sb[:], offs)
-        nc.sync.dma_start(offs2_sb[:], offs2)
-        nc.sync.dma_start(words[:], emb_words[0].rearrange("p u r -> p (u r)").bitcast(I32))
-
-        picked_rows = sb.tile([P, I], U8, name="picked_rows", align_bytes=64)
-        nc.vector.tensor_copy(picked_rows[:], scale_rows[:].indirect(offs_sb[:]))
         for q in range(4):
-            nc.scalar.dma_start(
-                emb_scale[32 * q : 32 * q + 4, :].bitcast(I32),
-                picked_rows[16 + 4 * q : 20 + 4 * q, :].bitcast(I32),
-            )
-
-        base_sb = sb.tile([P, PACK, T], F32, name="base_sb", tag="rows_then_base", align_bytes=64)
-        nc.sync.dma_start(base_sb[:], base.rearrange("(p j) t -> p j t", j=PACK))
+            nc.sync.dma_start(scale_rows[32 * q : 32 * q + 4, :].bitcast(I32), emb_scales[0, 4 * q : 4 * q + 4, :].bitcast(I32))
+        nc.sync.dma_start(offs_sb[:], offs)
+        nc.sync.dma_start(words[:], emb_words[0].rearrange("p u r -> p (u r)").bitcast(I32))
+        nc.sync.dma_start(offs2_sb[:], offs2)
+        nc.sync.dma_start(wo_raw[:], wo.rearrange("(p j) f -> p j f", j=PACK))
+        base_hbm = base.rearrange("(p j) t -> p j t", j=PACK)
+        for j in range(0, PACK, 2):
+            nc.sync.dma_start(base_sb[:, j : j + 2, :], base_hbm[:, j : j + 2, :])
 
         wv_dealt = sb.tile([P, PACK, P, PACK], BF16, name="wv_dealt", align_bytes=64)
         deal(nc.scalar.copy, wv_dealt, wv_raw, 0, 40)
         deal(nc.vector.tensor_copy, wv_dealt, wv_raw, 40, P)
+        emb_scale = sb.tile([P, I], U8, name="emb_scale", align_bytes=64)
+        nc.vector.tensor_copy(emb_scale[:], scale_rows[:].indirect(offs_sb[:]))
         wv_codes = sb.tile([P, E], U32, name="wv_codes", align_bytes=64)
         wv_scale = sb.tile([P, E], U8, name="wv_scale", align_bytes=64)
         nc.vector.quantize_mx(wv_codes[:].bitcast(FP8X4), wv_scale[:], wv_dealt[:].rearrange("p s m j -> p (s m j)"))
 
         emb_codes = sb.tile([P, I], U32, name="emb_codes", align_bytes=64)
         nc.vector.tensor_copy(emb_codes[:], words[:].bitcast(U32).indirect(offs_sb[:]))
-
-        wo_raw = sb.tile([P, PACK, F], F32, name="wo_raw", tag="words_then_wo", align_bytes=64)
-        nc.sync.dma_start(wo_raw[:], wo.rearrange("(p j) f -> p j f", j=PACK))
 
         pages = [sb.tile([P, T], F32, name="page%d" % j, align_bytes=64) for j in range(PACK)]
         for j in range(PACK):
@@ -97,7 +88,7 @@ def tile_attend_headpage_proj_pl_kernel(tc, emb_words, emb_scales, wv, base, wo,
             nc.scalar.copy(v_sb[:], v_ps[:])
             nc.vector.tensor_copy(pages[j][:].indirect(offs2_sb[:]), v_sb[:])
             if j < PACK - 1:
-                nc.gpsimd.tensor_tensor(x_planes[:, j, :], pages[j][:], base_sb[:, j, :], ADD)
+                nc.vector.tensor_tensor(x_planes[:, j, :], pages[j][:], base_sb[:, j, :], ADD)
 
         wo_dealt = sb.tile([P, PACK, P, PACK], BF16, name="wo_dealt", align_bytes=64)
         deal(nc.scalar.copy, wo_dealt, wo_raw, 0, P)
@@ -110,7 +101,7 @@ def tile_attend_headpage_proj_pl_kernel(tc, emb_words, emb_scales, wv, base, wo,
         y_scale = sb.tile([P, T], U8, name="y_scale", align_bytes=64)
         y_hbm = out_0.rearrange("(p s) t -> p s t", s=PACK)
         codes_hbm = out_1[0].rearrange("p t r -> p (t r)").bitcast(I32)
-        x_woven, x_codes, x_scale, y_ps, y_woven = {}, {}, {}, {}, {}
+        x_woven, x_codes, x_scale, y_bank, y_woven = {}, {}, {}, {}, {}
 
         def cols_of(c):
             return slice(CH * c, CH * (c + 1))
@@ -118,43 +109,60 @@ def tile_attend_headpage_proj_pl_kernel(tc, emb_words, emb_scales, wv, base, wo,
         def add_last(c):
             nc.vector.tensor_tensor(x_planes[:, 3, cols_of(c)], pages[3][:, cols_of(c)], base_sb[:, 3, cols_of(c)], ADD)
 
-        def weave_x(c):
+        def weave_x(c, engine_copy):
             x_woven[c] = sb.tile([P, CH, PACK], BF16, name="x_woven%d" % c, align_bytes=64)
-            weave(nc.vector.tensor_copy if c % 2 == 0 else nc.scalar.copy, x_woven[c][:], x_planes[:, :, cols_of(c)])
+            weave(engine_copy, x_woven[c][:], x_planes[:, :, cols_of(c)])
+
+        def quantize_x(c):
+            x_codes[c] = sb.tile([P, CH], U32, name="x_codes%d" % c, align_bytes=64)
+            x_scale[c] = sb.tile([P, CH], U8, name="x_scale%d" % c, align_bytes=64)
+            nc.vector.quantize_mx(x_codes[c][:].bitcast(FP8X4), x_scale[c][:], x_woven[c][:].rearrange("p t j -> p (t j)"))
 
         def project(c):
-            x_codes = sb.tile([P, CH], U32, name="x_codes%d" % c, align_bytes=64)
-            x_scale = sb.tile([P, CH], U8, name="x_scale%d" % c, align_bytes=64)
-            nc.vector.quantize_mx(x_codes[:].bitcast(FP8X4), x_scale[:], x_woven[c][:].rearrange("p t j -> p (t j)"))
             y_ps = ps.tile([P, PACK, CH], F32, name="y_ps%d" % c)
             for s in range(PACK):
                 cols = slice(P * s, P * (s + 1))
                 nc.tensor.matmul_mx(
                     y_ps[:, s, :], lhsT=wo_codes[:, cols].bitcast(FP8X4), lhsT_scale=wo_scale[:, cols],
-                    rhs=x_codes[:].bitcast(FP8X4), rhs_scale=x_scale[:], start=True, stop=True,
+                    rhs=x_codes[c][:].bitcast(FP8X4), rhs_scale=x_scale[c][:], start=True, stop=True,
                 )
-            nc.scalar.copy(y_sb[:, :, cols_of(c)], y_ps[:])
+            y_bank[c] = y_ps
+
+        def store_y(c):
+            nc.scalar.copy(y_sb[:, :, cols_of(c)], y_bank[c][:])
             nc.sync.dma_start(y_hbm[:, :, cols_of(c)], y_sb[:, :, cols_of(c)])
 
-        def weave_y(c):
+        def weave_y(c, planes):
             y_woven[c] = sb.tile([P, CH, PACK], BF16, name="y_woven%d" % c, align_bytes=64)
-            weave(nc.vector.tensor_copy, y_woven[c][:], y_sb[:, :, cols_of(c)])
+            weave(nc.vector.tensor_copy, y_woven[c][:], planes)
 
         def quantize_y(c):
             nc.vector.quantize_mx(y_codes[:, cols_of(c)].bitcast(FP8X4), y_scale[:, cols_of(c)], y_woven[c][:].rearrange("p t j -> p (t j)"))
 
-        for c in range(NCH):
-            add_last(c)
-        for c in range(NCH):
-            weave_x(c)
+        add_last(0)
+        add_last(1)
+        weave_x(0, nc.vector.tensor_copy)
+        weave_x(1, nc.scalar.copy)
+        add_last(2)
+        add_last(3)
+        quantize_x(0)
+        weave_x(2, nc.vector.tensor_copy)
+        weave_x(3, nc.scalar.copy)
+        for c in range(1, NCH):
+            quantize_x(c)
         for c in range(NCH):
             project(c)
-        for c in range(NCH):
-            weave_y(c)
-            if c > 0:
-                quantize_y(c - 1)
-        quantize_y(NCH - 1)
-        nc.sync.dma_start(codes_hbm, y_codes[:].bitcast(I32))
+        last = NCH - 1
+        for c in range(last):
+            store_y(c)
+            weave_y(c, y_sb[:, :, cols_of(c)])
+            quantize_y(c)
+        early = slice(0, CH * last)
+        nc.sync.dma_start(codes_hbm[:, early], y_codes[:, early].bitcast(I32))
+        store_y(last)
+        weave_y(last, y_sb[:, :, cols_of(last)])
+        quantize_y(last)
+        nc.scalar.dma_start(codes_hbm[:, cols_of(last)], y_codes[:, cols_of(last)].bitcast(I32))
         for q in range(4):
             queue = nc.scalar if q % 2 else nc.sync
             queue.dma_start(out_2[0, 4 * q : 4 * q + 4, :].bitcast(I32), y_scale[32 * q : 32 * q + 4, :].bitcast(I32))

@@ -20,10 +20,10 @@ CH = 128
 NCH = T // CH
 
 
-def deal(engine_copy, dealt, raw, m0, m1):
+def deal(engine_copy, dealt, raw, m0, m1, first):
     engine_copy(
-        dealt[:, :, m0:m1, :].rearrange("p s m j -> p m j s"),
-        raw[:, :, PACK * m0 : PACK * m1].rearrange("p j (m s) -> p m j s", s=PACK),
+        dealt[:, :, m0:m1, :],
+        raw[:, :, PACK * (m0 - first) : PACK * (m1 - first)].rearrange("p j (m s) -> p s m j", s=PACK),
     )
 
 
@@ -42,14 +42,16 @@ def tile_attend_headpage_proj_pl_kernel(tc, emb_words, emb_scales, wv, base, wo,
 
         offs_sb = sb.tile([P, I // 16], U16, name="offs_sb")
         offs2_sb = sb.tile([P, I // 16], U16, name="offs2_sb")
-        wv_raw = sb.tile([P, PACK, E], F32, name="wv_raw", align_bytes=64)
-        wo_raw = sb.tile([P, PACK, F], F32, name="wo_raw", align_bytes=64)
+        wv_raw = [sb.tile([P, PACK, E // 2], F32, name="wv_raw%d" % h, align_bytes=64) for h in range(2)]
+        wo_raw = sb.tile([P, PACK, F], F32, name="wo_raw", tag="x_woven0", align_bytes=64)
         base_sb = sb.tile([P, PACK, T], F32, name="base_sb", align_bytes=64)
         words = sb.tile([P, U], I32, name="words", align_bytes=64)
         scale_rows = sb.tile([P, U], U8, name="scale_rows", align_bytes=64)
 
         nc.vector.memset(scale_rows[:].bitcast(I32), 0)
-        nc.sync.dma_start(wv_raw[:], wv.rearrange("(p j) e -> p j e", j=PACK))
+        wv_hbm = wv.rearrange("(p j) e -> p j e", j=PACK)
+        for h in range(2):
+            nc.sync.dma_start(wv_raw[h][:], wv_hbm[:, :, E // 2 * h : E // 2 * (h + 1)])
         for q in range(4):
             nc.sync.dma_start(scale_rows[32 * q : 32 * q + 4, :].bitcast(I32), emb_scales[0, 4 * q : 4 * q + 4, :].bitcast(I32))
         nc.sync.dma_start(offs_sb[:], offs)
@@ -61,8 +63,10 @@ def tile_attend_headpage_proj_pl_kernel(tc, emb_words, emb_scales, wv, base, wo,
             nc.sync.dma_start(base_sb[:, j : j + 2, :], base_hbm[:, j : j + 2, :])
 
         wv_dealt = sb.tile([P, PACK, P, PACK], BF16, name="wv_dealt", align_bytes=64)
-        deal(nc.scalar.copy, wv_dealt, wv_raw, 0, 40)
-        deal(nc.vector.tensor_copy, wv_dealt, wv_raw, 40, P)
+        for h in range(2):
+            first = P // 2 * h
+            deal(nc.vector.tensor_copy, wv_dealt, wv_raw[h], first, first + 44, first)
+            deal(nc.scalar.copy, wv_dealt, wv_raw[h], first + 44, first + P // 2, first)
         emb_scale = sb.tile([P, I], U8, name="emb_scale", align_bytes=64)
         nc.vector.tensor_copy(emb_scale[:], scale_rows[:].indirect(offs_sb[:]))
         wv_codes = sb.tile([P, E], U32, name="wv_codes", align_bytes=64)
@@ -88,13 +92,19 @@ def tile_attend_headpage_proj_pl_kernel(tc, emb_words, emb_scales, wv, base, wo,
             nc.scalar.copy(v_sb[:], v_ps[:])
             nc.vector.tensor_copy(pages[j][:].indirect(offs2_sb[:]), v_sb[:])
             if j < PACK - 1:
-                nc.vector.tensor_tensor(x_planes[:, j, :], pages[j][:], base_sb[:, j, :], ADD)
+                nc.gpsimd.tensor_tensor(x_planes[:, j, :], pages[j][:], base_sb[:, j, :], ADD)
 
         wo_dealt = sb.tile([P, PACK, P, PACK], BF16, name="wo_dealt", align_bytes=64)
-        deal(nc.scalar.copy, wo_dealt, wo_raw, 0, P)
+        deal(nc.scalar.copy, wo_dealt, wo_raw, 0, P, 0)
         wo_codes = sb.tile([P, F], U32, name="wo_codes", align_bytes=64)
         wo_scale = sb.tile([P, F], U8, name="wo_scale", align_bytes=64)
-        nc.vector.quantize_mx(wo_codes[:].bitcast(FP8X4), wo_scale[:], wo_dealt[:].rearrange("p s m j -> p (s m j)"))
+
+        def quantize_wo(h):
+            cols = slice(F // 2 * h, F // 2 * (h + 1))
+            nc.vector.quantize_mx(
+                wo_codes[:, cols].bitcast(FP8X4), wo_scale[:, cols],
+                wo_dealt[:, 2 * h : 2 * h + 2].rearrange("p s m j -> p (s m j)"),
+            )
 
         y_sb = sb.tile([P, PACK, T], F32, name="y_sb", align_bytes=64)
         y_codes = sb.tile([P, T], U32, name="y_codes", align_bytes=64)
@@ -106,11 +116,12 @@ def tile_attend_headpage_proj_pl_kernel(tc, emb_words, emb_scales, wv, base, wo,
         def cols_of(c):
             return slice(CH * c, CH * (c + 1))
 
-        def add_last(c):
-            nc.vector.tensor_tensor(x_planes[:, 3, cols_of(c)], pages[3][:, cols_of(c)], base_sb[:, 3, cols_of(c)], ADD)
+        def add_last(c0, c1):
+            cols = slice(CH * c0, CH * c1)
+            nc.vector.tensor_tensor(x_planes[:, 3, cols], pages[3][:, cols], base_sb[:, 3, cols], ADD)
 
         def weave_x(c, engine_copy):
-            x_woven[c] = sb.tile([P, CH, PACK], BF16, name="x_woven%d" % c, align_bytes=64)
+            x_woven[c] = sb.tile([P, CH, PACK], BF16, name="x_woven%d" % c, tag="x_woven%d" % c, align_bytes=64)
             weave(engine_copy, x_woven[c][:], x_planes[:, :, cols_of(c)])
 
         def quantize_x(c):
@@ -139,17 +150,19 @@ def tile_attend_headpage_proj_pl_kernel(tc, emb_words, emb_scales, wv, base, wo,
         def quantize_y(c):
             nc.vector.quantize_mx(y_codes[:, cols_of(c)].bitcast(FP8X4), y_scale[:, cols_of(c)], y_woven[c][:].rearrange("p t j -> p (t j)"))
 
-        add_last(0)
-        add_last(1)
+        add_last(0, 1)
+        add_last(1, 2)
+        add_last(2, 4)
         weave_x(0, nc.vector.tensor_copy)
         weave_x(1, nc.scalar.copy)
-        add_last(2)
-        add_last(3)
+        weave_x(2, nc.scalar.copy)
+        quantize_wo(0)
         quantize_x(0)
-        weave_x(2, nc.vector.tensor_copy)
-        weave_x(3, nc.scalar.copy)
-        for c in range(1, NCH):
-            quantize_x(c)
+        quantize_wo(1)
+        quantize_x(1)
+        weave_x(3, nc.vector.tensor_copy)
+        quantize_x(2)
+        quantize_x(3)
         for c in range(NCH):
             project(c)
         last = NCH - 1

@@ -1,6 +1,7 @@
 from contextlib import ExitStack
 
 import concourse.mybir as mybir
+from concourse.masks import make_identity
 
 K, U, I, T, E, F = 512, 2048, 256, 512, 512, 512
 FLOPS = 2 * K * E * I + 2 * E * F * T
@@ -27,6 +28,13 @@ def deal(engine_copy, dealt, raw, m0, m1, first):
     )
 
 
+def deal_pairs(engine_copy, dealt, raw):
+    engine_copy(
+        dealt.rearrange("p (a b) m j -> p a m j b", b=2),
+        raw.rearrange("p j (m a b) -> p a m j b", a=2, b=2),
+    )
+
+
 def weave(engine_copy, woven, planes):
     engine_copy(
         woven.rearrange("p (c i) j -> p c j i", i=4),
@@ -43,8 +51,8 @@ def tile_attend_headpage_proj_pl_kernel(tc, emb_words, emb_scales, wv, base, wo,
         offs_sb = sb.tile([P, I // 16], U16, name="offs_sb")
         offs2_sb = sb.tile([P, I // 16], U16, name="offs2_sb")
         wv_raw = [sb.tile([P, PACK, E // 2], F32, name="wv_raw%d" % h, align_bytes=64) for h in range(2)]
-        wo_raw = sb.tile([P, PACK, F], F32, name="wo_raw", tag="x_woven0", align_bytes=64)
-        base_sb = sb.tile([P, PACK, T], F32, name="base_sb", align_bytes=64)
+        wo_raw = sb.tile([P, PACK, F], F32, name="wo_raw", align_bytes=64)
+        base_sb = [sb.tile([P, 2, T], F32, name="base_sb%d" % h, align_bytes=64) for h in range(2)]
         words = sb.tile([P, U], I32, name="words", align_bytes=64)
         scale_rows = sb.tile([P, U], U8, name="scale_rows", align_bytes=64)
 
@@ -59,8 +67,8 @@ def tile_attend_headpage_proj_pl_kernel(tc, emb_words, emb_scales, wv, base, wo,
         nc.sync.dma_start(offs2_sb[:], offs2)
         nc.sync.dma_start(wo_raw[:], wo.rearrange("(p j) f -> p j f", j=PACK))
         base_hbm = base.rearrange("(p j) t -> p j t", j=PACK)
-        for j in range(0, PACK, 2):
-            nc.sync.dma_start(base_sb[:, j : j + 2, :], base_hbm[:, j : j + 2, :])
+        for h in range(2):
+            nc.sync.dma_start(base_sb[h][:], base_hbm[:, 2 * h : 2 * h + 2, :])
 
         wv_dealt = sb.tile([P, PACK, P, PACK], BF16, name="wv_dealt", align_bytes=64)
         for h in range(2):
@@ -76,14 +84,19 @@ def tile_attend_headpage_proj_pl_kernel(tc, emb_words, emb_scales, wv, base, wo,
         emb_codes = sb.tile([P, I], U32, name="emb_codes", align_bytes=64)
         nc.vector.tensor_copy(emb_codes[:], words[:].bitcast(U32).indirect(offs_sb[:]))
 
-        pages = [sb.tile([P, T], F32, name="page%d" % j, align_bytes=64) for j in range(PACK)]
+        pages = [sb.tile([P, T], F32, name="page%d" % j, tag="page%d" % j, align_bytes=64) for j in range(PACK)]
         for j in range(PACK):
             nc.vector.memset(pages[j][:], 0.0)
+
+        ident = sb.tile([P, P], F32, name="ident", align_bytes=64)
+        ident_bf = sb.tile([P, P], BF16, name="ident_bf", align_bytes=64)
+        make_identity(nc, ident[:])
+        make_identity(nc, ident_bf[:])
 
         x_planes = sb.tile([P, PACK, T], BF16, name="x_planes", align_bytes=64)
         for j in range(PACK):
             cols = slice(P * j, P * (j + 1))
-            v_ps = ps.tile([P, I], F32, name="v_ps%d" % j)
+            v_ps = ps.tile([P, I], F32, name="v_ps%d" % j, tag="bank%d" % j)
             nc.tensor.matmul_mx(
                 v_ps[:], lhsT=wv_codes[:, cols].bitcast(FP8X4), lhsT_scale=wv_scale[:, cols],
                 rhs=emb_codes[:].bitcast(FP8X4), rhs_scale=emb_scale[:], start=True, stop=True,
@@ -91,18 +104,32 @@ def tile_attend_headpage_proj_pl_kernel(tc, emb_words, emb_scales, wv, base, wo,
             v_sb = sb.tile([P, I], F32, name="v_sb%d" % j, align_bytes=64)
             nc.scalar.copy(v_sb[:], v_ps[:])
             nc.vector.tensor_copy(pages[j][:].indirect(offs2_sb[:]), v_sb[:])
-            if j < PACK - 1:
-                nc.gpsimd.tensor_tensor(x_planes[:, j, :], pages[j][:], base_sb[:, j, :], ADD)
 
         wo_dealt = sb.tile([P, PACK, P, PACK], BF16, name="wo_dealt", align_bytes=64)
-        deal(nc.scalar.copy, wo_dealt, wo_raw, 0, P, 0)
-        wo_codes = sb.tile([P, F], U32, name="wo_codes", align_bytes=64)
+        deal_pairs(nc.scalar.copy, wo_dealt[:], wo_raw[:])
+        turned = []
+        for j in range(2):
+            sum_ps = ps.tile([P, NCH, P], F32, name="sum_ps%d" % j)
+            for c in range(NCH):
+                cols = slice(P * c, P * (c + 1))
+                nc.tensor.matmul(sum_ps[:, c, :], lhsT=base_sb[0][:, j, cols], rhs=ident[:], is_transpose=True, start=True, stop=False)
+                nc.tensor.matmul(sum_ps[:, c, :], lhsT=pages[j][:, cols], rhs=ident[:], is_transpose=True, start=False, stop=True)
+            turned.append(sb.tile([P, NCH, P], BF16, name="turned%d" % j, align_bytes=64))
+            nc.scalar.copy(turned[j][:], sum_ps[:])
+        for j in range(2):
+            back_ps = ps.tile([P, T], BF16, name="back_ps%d" % j)
+            for c in range(NCH):
+                nc.tensor.transpose(back_ps[:, P * c : P * (c + 1)], turned[j][:, c, :], ident_bf[:])
+            nc.scalar.copy(x_planes[:, j, :], back_ps[:])
+
+        wo_codes = {}
         wo_scale = sb.tile([P, F], U8, name="wo_scale", align_bytes=64)
 
         def quantize_wo(h):
             cols = slice(F // 2 * h, F // 2 * (h + 1))
+            wo_codes[h] = sb.tile([P, F // 2], U32, name="wo_codes%d" % h, tag=("page2", "x_woven0")[h], align_bytes=64)
             nc.vector.quantize_mx(
-                wo_codes[:, cols].bitcast(FP8X4), wo_scale[:, cols],
+                wo_codes[h][:].bitcast(FP8X4), wo_scale[:, cols],
                 wo_dealt[:, 2 * h : 2 * h + 2].rearrange("p s m j -> p (s m j)"),
             )
 
@@ -118,7 +145,8 @@ def tile_attend_headpage_proj_pl_kernel(tc, emb_words, emb_scales, wv, base, wo,
 
         def add_last(c0, c1):
             cols = slice(CH * c0, CH * c1)
-            nc.vector.tensor_tensor(x_planes[:, 3, cols], pages[3][:, cols], base_sb[:, 3, cols], ADD)
+            for j in (2, 3):
+                nc.vector.tensor_tensor(x_planes[:, j, cols], pages[j][:, cols], base_sb[1][:, j - 2, cols], ADD)
 
         def weave_x(c, engine_copy):
             x_woven[c] = sb.tile([P, CH, PACK], BF16, name="x_woven%d" % c, tag="x_woven%d" % c, align_bytes=64)
@@ -130,17 +158,17 @@ def tile_attend_headpage_proj_pl_kernel(tc, emb_words, emb_scales, wv, base, wo,
             nc.vector.quantize_mx(x_codes[c][:].bitcast(FP8X4), x_scale[c][:], x_woven[c][:].rearrange("p t j -> p (t j)"))
 
         def project(c):
-            y_ps = ps.tile([P, PACK, CH], F32, name="y_ps%d" % c)
+            y_ps = ps.tile([P, PACK, CH], F32, name="y_ps%d" % c, tag="bank%d" % c)
             for s in range(PACK):
                 cols = slice(P * s, P * (s + 1))
                 nc.tensor.matmul_mx(
-                    y_ps[:, s, :], lhsT=wo_codes[:, cols].bitcast(FP8X4), lhsT_scale=wo_scale[:, cols],
+                    y_ps[:, s, :], lhsT=wo_codes[s // 2][:, P * (s % 2) : P * (s % 2 + 1)].bitcast(FP8X4), lhsT_scale=wo_scale[:, cols],
                     rhs=x_codes[c][:].bitcast(FP8X4), rhs_scale=x_scale[c][:], start=True, stop=True,
                 )
             y_bank[c] = y_ps
 
-        def store_y(c):
-            nc.scalar.copy(y_sb[:, :, cols_of(c)], y_bank[c][:])
+        def store_y(c, engine_copy=nc.scalar.copy):
+            engine_copy(y_sb[:, :, cols_of(c)], y_bank[c][:])
             nc.sync.dma_start(y_hbm[:, :, cols_of(c)], y_sb[:, :, cols_of(c)])
 
         def weave_y(c, planes):
@@ -153,16 +181,13 @@ def tile_attend_headpage_proj_pl_kernel(tc, emb_words, emb_scales, wv, base, wo,
         add_last(0, 1)
         add_last(1, 2)
         add_last(2, 4)
-        weave_x(0, nc.vector.tensor_copy)
-        weave_x(1, nc.scalar.copy)
-        weave_x(2, nc.scalar.copy)
         quantize_wo(0)
+        for c in range(NCH):
+            weave_x(c, nc.scalar.copy)
         quantize_x(0)
         quantize_wo(1)
-        quantize_x(1)
-        weave_x(3, nc.vector.tensor_copy)
-        quantize_x(2)
-        quantize_x(3)
+        for c in range(1, NCH):
+            quantize_x(c)
         for c in range(NCH):
             project(c)
         last = NCH - 1

@@ -17,18 +17,16 @@ ADD = mybir.AluOpType.add
 
 P = 128
 PACK = 4
-CH = 128
-NCH = T // CH
+QUADRANTS = 4
+LIST_ROWS = 16
+CHUNK = 128
+CHUNKS = T // CHUNK
+LAST = CHUNKS - 1
+TURNED_PLANES = 2
+VECTOR_SHARE = 88
 
 
-def deal(engine_copy, dealt, raw, m0, m1, first):
-    engine_copy(
-        dealt[:, :, m0:m1, :],
-        raw[:, :, PACK * (m0 - first) : PACK * (m1 - first)].rearrange("p j (m s) -> p s m j", s=PACK),
-    )
-
-
-def deal_pairs(engine_copy, dealt, raw):
+def deal(engine_copy, dealt, raw):
     engine_copy(
         dealt.rearrange("p (a b) m j -> p a m j b", b=2),
         raw.rearrange("p j (m a b) -> p a m j b", a=2, b=2),
@@ -42,25 +40,27 @@ def weave(engine_copy, woven, planes):
     )
 
 
+def chunk_cols(first, stop):
+    return slice(CHUNK * first, CHUNK * stop)
+
+
 def tile_attend_headpage_proj_pl_kernel(tc, emb_words, emb_scales, wv, base, wo, offs, offs2, out_0, out_1, out_2):
     nc = tc.nc
     with ExitStack() as ctx:
         sb = ctx.enter_context(tc.tile_pool(name="sb", bufs=1))
         ps = ctx.enter_context(tc.psum_pool(name="ps", bufs=1))
 
-        offs_sb = sb.tile([P, I // 16], U16, name="offs_sb")
-        offs2_sb = sb.tile([P, I // 16], U16, name="offs2_sb")
-        wv_raw = [sb.tile([P, PACK, E // 2], F32, name="wv_raw%d" % h, align_bytes=64) for h in range(2)]
+        offs_sb = sb.tile([P, I // LIST_ROWS], U16, name="offs_sb")
+        offs2_sb = sb.tile([P, I // LIST_ROWS], U16, name="offs2_sb")
+        wv_raw = sb.tile([P, PACK, E], F32, name="wv_raw", align_bytes=64)
         wo_raw = sb.tile([P, PACK, F], F32, name="wo_raw", align_bytes=64)
         base_sb = [sb.tile([P, 2, T], F32, name="base_sb%d" % h, align_bytes=64) for h in range(2)]
         words = sb.tile([P, U], I32, name="words", align_bytes=64)
         scale_rows = sb.tile([P, U], U8, name="scale_rows", align_bytes=64)
 
         nc.vector.memset(scale_rows[:].bitcast(I32), 0)
-        wv_hbm = wv.rearrange("(p j) e -> p j e", j=PACK)
-        for h in range(2):
-            nc.sync.dma_start(wv_raw[h][:], wv_hbm[:, :, E // 2 * h : E // 2 * (h + 1)])
-        for q in range(4):
+        nc.sync.dma_start(wv_raw[:], wv.rearrange("(p j) e -> p j e", j=PACK))
+        for q in range(QUADRANTS):
             nc.sync.dma_start(scale_rows[32 * q : 32 * q + 4, :].bitcast(I32), emb_scales[0, 4 * q : 4 * q + 4, :].bitcast(I32))
         nc.sync.dma_start(offs_sb[:], offs)
         nc.sync.dma_start(words[:], emb_words[0].rearrange("p u r -> p (u r)").bitcast(I32))
@@ -71,10 +71,8 @@ def tile_attend_headpage_proj_pl_kernel(tc, emb_words, emb_scales, wv, base, wo,
             nc.sync.dma_start(base_sb[h][:], base_hbm[:, 2 * h : 2 * h + 2, :])
 
         wv_dealt = sb.tile([P, PACK, P, PACK], BF16, name="wv_dealt", align_bytes=64)
-        for h in range(2):
-            first = P // 2 * h
-            deal(nc.vector.tensor_copy, wv_dealt, wv_raw[h], first, first + 44, first)
-            deal(nc.scalar.copy, wv_dealt, wv_raw[h], first + 44, first + P // 2, first)
+        deal(nc.vector.tensor_copy, wv_dealt[:, :, :VECTOR_SHARE, :], wv_raw[:, :, : PACK * VECTOR_SHARE])
+        deal(nc.scalar.copy, wv_dealt[:, :, VECTOR_SHARE:, :], wv_raw[:, :, PACK * VECTOR_SHARE :])
         emb_scale = sb.tile([P, I], U8, name="emb_scale", align_bytes=64)
         nc.vector.tensor_copy(emb_scale[:], scale_rows[:].indirect(offs_sb[:]))
         wv_codes = sb.tile([P, E], U32, name="wv_codes", align_bytes=64)
@@ -95,10 +93,10 @@ def tile_attend_headpage_proj_pl_kernel(tc, emb_words, emb_scales, wv, base, wo,
 
         x_planes = sb.tile([P, PACK, T], BF16, name="x_planes", align_bytes=64)
         for j in range(PACK):
-            cols = slice(P * j, P * (j + 1))
+            plane_cols = slice(P * j, P * (j + 1))
             v_ps = ps.tile([P, I], F32, name="v_ps%d" % j, tag="bank%d" % j)
             nc.tensor.matmul_mx(
-                v_ps[:], lhsT=wv_codes[:, cols].bitcast(FP8X4), lhsT_scale=wv_scale[:, cols],
+                v_ps[:], lhsT=wv_codes[:, plane_cols].bitcast(FP8X4), lhsT_scale=wv_scale[:, plane_cols],
                 rhs=emb_codes[:].bitcast(FP8X4), rhs_scale=emb_scale[:], start=True, stop=True,
             )
             v_sb = sb.tile([P, I], F32, name="v_sb%d" % j, align_bytes=64)
@@ -106,101 +104,90 @@ def tile_attend_headpage_proj_pl_kernel(tc, emb_words, emb_scales, wv, base, wo,
             nc.vector.tensor_copy(pages[j][:].indirect(offs2_sb[:]), v_sb[:])
 
         wo_dealt = sb.tile([P, PACK, P, PACK], BF16, name="wo_dealt", align_bytes=64)
-        deal_pairs(nc.scalar.copy, wo_dealt[:], wo_raw[:])
+        deal(nc.scalar.copy, wo_dealt[:], wo_raw[:])
+
         turned = []
-        for j in range(2):
-            sum_ps = ps.tile([P, NCH, P], F32, name="sum_ps%d" % j)
-            for c in range(NCH):
-                cols = slice(P * c, P * (c + 1))
+        for j in range(TURNED_PLANES):
+            sum_ps = ps.tile([P, CHUNKS, P], F32, name="sum_ps%d" % j)
+            for c in range(CHUNKS):
+                cols = chunk_cols(c, c + 1)
                 nc.tensor.matmul(sum_ps[:, c, :], lhsT=base_sb[0][:, j, cols], rhs=ident[:], is_transpose=True, start=True, stop=False)
                 nc.tensor.matmul(sum_ps[:, c, :], lhsT=pages[j][:, cols], rhs=ident[:], is_transpose=True, start=False, stop=True)
-            turned.append(sb.tile([P, NCH, P], BF16, name="turned%d" % j, align_bytes=64))
+            turned.append(sb.tile([P, CHUNKS, P], BF16, name="turned%d" % j, align_bytes=64))
             nc.scalar.copy(turned[j][:], sum_ps[:])
-        for j in range(2):
+        for j in range(TURNED_PLANES):
             back_ps = ps.tile([P, T], BF16, name="back_ps%d" % j)
-            for c in range(NCH):
-                nc.tensor.transpose(back_ps[:, P * c : P * (c + 1)], turned[j][:, c, :], ident_bf[:])
+            for c in range(CHUNKS):
+                nc.tensor.transpose(back_ps[:, chunk_cols(c, c + 1)], turned[j][:, c, :], ident_bf[:])
             nc.scalar.copy(x_planes[:, j, :], back_ps[:])
 
-        wo_codes = {}
         wo_scale = sb.tile([P, F], U8, name="wo_scale", align_bytes=64)
-
-        def quantize_wo(h):
-            cols = slice(F // 2 * h, F // 2 * (h + 1))
-            wo_codes[h] = sb.tile([P, F // 2], U32, name="wo_codes%d" % h, tag=("page2", "x_woven0")[h], align_bytes=64)
-            nc.vector.quantize_mx(
-                wo_codes[h][:].bitcast(FP8X4), wo_scale[:, cols],
-                wo_dealt[:, 2 * h : 2 * h + 2].rearrange("p s m j -> p (s m j)"),
-            )
-
         y_sb = sb.tile([P, PACK, T], F32, name="y_sb", align_bytes=64)
         y_codes = sb.tile([P, T], U32, name="y_codes", align_bytes=64)
         y_scale = sb.tile([P, T], U8, name="y_scale", align_bytes=64)
         y_hbm = out_0.rearrange("(p s) t -> p s t", s=PACK)
         codes_hbm = out_1[0].rearrange("p t r -> p (t r)").bitcast(I32)
-        x_woven, x_codes, x_scale, y_bank, y_woven = {}, {}, {}, {}, {}
+        wo_codes, x_woven, x_codes, x_scale, y_ps = {}, {}, {}, {}, {}
 
-        def cols_of(c):
-            return slice(CH * c, CH * (c + 1))
+        def add_base(cols):
+            for j in range(TURNED_PLANES, PACK):
+                nc.vector.tensor_tensor(x_planes[:, j, cols], pages[j][:, cols], base_sb[1][:, j - TURNED_PLANES, cols], ADD)
 
-        def add_last(c0, c1):
-            cols = slice(CH * c0, CH * c1)
-            for j in (2, 3):
-                nc.vector.tensor_tensor(x_planes[:, j, cols], pages[j][:, cols], base_sb[1][:, j - 2, cols], ADD)
+        def quantize_wo(h, reused_tag):
+            wo_codes[h] = sb.tile([P, F // 2], U32, name="wo_codes%d" % h, tag=reused_tag, align_bytes=64)
+            nc.vector.quantize_mx(
+                wo_codes[h][:].bitcast(FP8X4), wo_scale[:, F // 2 * h : F // 2 * (h + 1)],
+                wo_dealt[:, 2 * h : 2 * h + 2].rearrange("p s m j -> p (s m j)"),
+            )
 
-        def weave_x(c, engine_copy):
-            x_woven[c] = sb.tile([P, CH, PACK], BF16, name="x_woven%d" % c, tag="x_woven%d" % c, align_bytes=64)
-            weave(engine_copy, x_woven[c][:], x_planes[:, :, cols_of(c)])
+        def weave_x(c, engine_copy, tag):
+            x_woven[c] = sb.tile([P, CHUNK, PACK], BF16, name="x_woven%d" % c, tag=tag, align_bytes=64)
+            weave(engine_copy, x_woven[c][:], x_planes[:, :, chunk_cols(c, c + 1)])
 
         def quantize_x(c):
-            x_codes[c] = sb.tile([P, CH], U32, name="x_codes%d" % c, align_bytes=64)
-            x_scale[c] = sb.tile([P, CH], U8, name="x_scale%d" % c, align_bytes=64)
+            x_codes[c] = sb.tile([P, CHUNK], U32, name="x_codes%d" % c, align_bytes=64)
+            x_scale[c] = sb.tile([P, CHUNK], U8, name="x_scale%d" % c, align_bytes=64)
             nc.vector.quantize_mx(x_codes[c][:].bitcast(FP8X4), x_scale[c][:], x_woven[c][:].rearrange("p t j -> p (t j)"))
 
         def project(c):
-            y_ps = ps.tile([P, PACK, CH], F32, name="y_ps%d" % c, tag="bank%d" % c)
+            y_ps[c] = ps.tile([P, PACK, CHUNK], F32, name="y_ps%d" % c, tag="bank%d" % c)
             for s in range(PACK):
-                cols = slice(P * s, P * (s + 1))
                 nc.tensor.matmul_mx(
-                    y_ps[:, s, :], lhsT=wo_codes[s // 2][:, P * (s % 2) : P * (s % 2 + 1)].bitcast(FP8X4), lhsT_scale=wo_scale[:, cols],
+                    y_ps[c][:, s, :],
+                    lhsT=wo_codes[s // 2][:, P * (s % 2) : P * (s % 2 + 1)].bitcast(FP8X4),
+                    lhsT_scale=wo_scale[:, P * s : P * (s + 1)],
                     rhs=x_codes[c][:].bitcast(FP8X4), rhs_scale=x_scale[c][:], start=True, stop=True,
                 )
-            y_bank[c] = y_ps
 
-        def store_y(c, engine_copy=nc.scalar.copy):
-            engine_copy(y_sb[:, :, cols_of(c)], y_bank[c][:])
-            nc.sync.dma_start(y_hbm[:, :, cols_of(c)], y_sb[:, :, cols_of(c)])
+        def hand_out(c):
+            cols = chunk_cols(c, c + 1)
+            nc.scalar.copy(y_sb[:, :, cols], y_ps[c][:])
+            nc.sync.dma_start(y_hbm[:, :, cols], y_sb[:, :, cols])
+            y_woven = sb.tile([P, CHUNK, PACK], BF16, name="y_woven%d" % c, align_bytes=64)
+            weave(nc.vector.tensor_copy, y_woven[:], y_sb[:, :, cols])
+            nc.vector.quantize_mx(y_codes[:, cols].bitcast(FP8X4), y_scale[:, cols], y_woven[:].rearrange("p t j -> p (t j)"))
 
-        def weave_y(c, planes):
-            y_woven[c] = sb.tile([P, CH, PACK], BF16, name="y_woven%d" % c, align_bytes=64)
-            weave(nc.vector.tensor_copy, y_woven[c][:], planes)
-
-        def quantize_y(c):
-            nc.vector.quantize_mx(y_codes[:, cols_of(c)].bitcast(FP8X4), y_scale[:, cols_of(c)], y_woven[c][:].rearrange("p t j -> p (t j)"))
-
-        add_last(0, 1)
-        add_last(1, 2)
-        add_last(2, 4)
-        quantize_wo(0)
-        for c in range(NCH):
-            weave_x(c, nc.scalar.copy)
+        add_base(chunk_cols(0, 1))
+        add_base(chunk_cols(1, 2))
+        add_base(chunk_cols(2, CHUNKS))
+        quantize_wo(0, "page2")
+        for c in range(LAST):
+            weave_x(c, nc.scalar.copy, "x_woven%d" % c)
         quantize_x(0)
-        quantize_wo(1)
-        for c in range(1, NCH):
+        quantize_wo(1, "x_woven0")
+        for c in range(1, LAST):
             quantize_x(c)
-        for c in range(NCH):
+        weave_x(LAST, nc.vector.tensor_copy, "x_woven1")
+        quantize_x(LAST)
+        for c in range(CHUNKS):
             project(c)
-        last = NCH - 1
-        for c in range(last):
-            store_y(c)
-            weave_y(c, y_sb[:, :, cols_of(c)])
-            quantize_y(c)
-        early = slice(0, CH * last)
+
+        for c in range(LAST):
+            hand_out(c)
+        early, late = chunk_cols(0, LAST), chunk_cols(LAST, CHUNKS)
         nc.sync.dma_start(codes_hbm[:, early], y_codes[:, early].bitcast(I32))
-        store_y(last)
-        weave_y(last, y_sb[:, :, cols_of(last)])
-        quantize_y(last)
-        nc.scalar.dma_start(codes_hbm[:, cols_of(last)], y_codes[:, cols_of(last)].bitcast(I32))
-        for q in range(4):
+        hand_out(LAST)
+        nc.scalar.dma_start(codes_hbm[:, late], y_codes[:, late].bitcast(I32))
+        for q in range(QUADRANTS):
             queue = nc.scalar if q % 2 else nc.sync
             queue.dma_start(out_2[0, 4 * q : 4 * q + 4, :].bitcast(I32), y_scale[32 * q : 32 * q + 4, :].bitcast(I32))

@@ -53,34 +53,41 @@ def tile_attend_headpage_proj_pl_kernel(tc, emb_words, emb_scales, wv, base, wo,
         offs_sb = sb.tile([P, I // LIST_ROWS], U16, name="offs_sb")
         offs2_sb = sb.tile([P, I // LIST_ROWS], U16, name="offs2_sb")
         wv_raw = sb.tile([P, PACK, E], F32, name="wv_raw", align_bytes=64)
-        wo_raw = sb.tile([P, PACK, F], F32, name="wo_raw", align_bytes=64)
+        wo_raw = sb.tile([P, PACK, F], F32, name="wo_raw", tag="wo_raw", align_bytes=64)
         base_sb = [sb.tile([P, 2, T], F32, name="base_sb%d" % h, align_bytes=64) for h in range(2)]
-        words = sb.tile([P, U], I32, name="words", align_bytes=64)
+        words = sb.tile([P, U], I32, name="words", tag="words", align_bytes=64)
         scale_rows = sb.tile([P, U], U8, name="scale_rows", align_bytes=64)
 
         nc.vector.memset(scale_rows[:].bitcast(I32), 0)
         nc.sync.dma_start(wv_raw[:], wv.rearrange("(p j) e -> p j e", j=PACK))
-        for q in range(QUADRANTS):
-            nc.sync.dma_start(scale_rows[32 * q : 32 * q + 4, :].bitcast(I32), emb_scales[0, 4 * q : 4 * q + 4, :].bitcast(I32))
+        for r in range(PACK):
+            nc.sync.dma_start(scale_rows[r:P:32, :].bitcast(I32), emb_scales[0, r : 16 : PACK, :].bitcast(I32))
         nc.sync.dma_start(offs_sb[:], offs)
         nc.sync.dma_start(words[:], emb_words[0].rearrange("p u r -> p (u r)").bitcast(I32))
         nc.sync.dma_start(offs2_sb[:], offs2)
-        nc.sync.dma_start(wo_raw[:], wo.rearrange("(p j) f -> p j f", j=PACK))
         base_hbm = base.rearrange("(p j) t -> p j t", j=PACK)
-        for h in range(2):
-            nc.sync.dma_start(base_sb[h][:], base_hbm[:, 2 * h : 2 * h + 2, :])
+        nc.sync.dma_start(base_sb[0][:], base_hbm[:, 0:2, :])
+        nc.sync.dma_start(wo_raw[:], wo.rearrange("(p j) f -> p j f", j=PACK))
+        nc.sync.dma_start(base_sb[1][:], base_hbm[:, 2:4, :])
 
         wv_dealt = sb.tile([P, PACK, P, PACK], BF16, name="wv_dealt", align_bytes=64)
         deal(nc.vector.tensor_copy, wv_dealt[:, :, :VECTOR_SHARE, :], wv_raw[:, :, : PACK * VECTOR_SHARE])
         deal(nc.scalar.copy, wv_dealt[:, :, VECTOR_SHARE:, :], wv_raw[:, :, PACK * VECTOR_SHARE :])
         emb_scale = sb.tile([P, I], U8, name="emb_scale", align_bytes=64)
         nc.vector.tensor_copy(emb_scale[:], scale_rows[:].indirect(offs_sb[:]))
-        wv_codes = sb.tile([P, E], U32, name="wv_codes", align_bytes=64)
-        wv_scale = sb.tile([P, E], U8, name="wv_scale", align_bytes=64)
-        nc.vector.quantize_mx(wv_codes[:].bitcast(FP8X4), wv_scale[:], wv_dealt[:].rearrange("p s m j -> p (s m j)"))
+        wv_codes, wv_scale = {}, {}
 
+        def quantize_wv(h, tag):
+            wv_codes[h] = sb.tile([P, E // 2], U32, name="wv_codes%d" % h, tag=tag, align_bytes=64)
+            wv_scale[h] = sb.tile([P, E // 2], U8, name="wv_scale%d" % h, align_bytes=64)
+            nc.vector.quantize_mx(
+                wv_codes[h][:].bitcast(FP8X4), wv_scale[h][:], wv_dealt[:, 2 * h : 2 * h + 2].rearrange("p s m j -> p (s m j)")
+            )
+
+        quantize_wv(0, "wv_codes0")
         emb_codes = sb.tile([P, I], U32, name="emb_codes", align_bytes=64)
         nc.vector.tensor_copy(emb_codes[:], words[:].bitcast(U32).indirect(offs_sb[:]))
+        quantize_wv(1, "words")
 
         pages = [sb.tile([P, T], F32, name="page%d" % j, tag="page%d" % j, align_bytes=64) for j in range(PACK)]
         for j in range(PACK):
@@ -92,33 +99,47 @@ def tile_attend_headpage_proj_pl_kernel(tc, emb_words, emb_scales, wv, base, wo,
         make_identity(nc, ident_bf[:])
 
         x_planes = sb.tile([P, PACK, T], BF16, name="x_planes", align_bytes=64)
-        for j in range(PACK):
-            plane_cols = slice(P * j, P * (j + 1))
-            v_ps = ps.tile([P, I], F32, name="v_ps%d" % j, tag="bank%d" % j)
+
+        def place_v(j, first, stop, tag):
+            plane_cols = slice(P * (j % 2), P * (j % 2 + 1))
+            v_ps = ps.tile([P, stop - first], F32, name="v_ps%d_%d" % (j, first), tag=tag)
             nc.tensor.matmul_mx(
-                v_ps[:], lhsT=wv_codes[:, plane_cols].bitcast(FP8X4), lhsT_scale=wv_scale[:, plane_cols],
-                rhs=emb_codes[:].bitcast(FP8X4), rhs_scale=emb_scale[:], start=True, stop=True,
+                v_ps[:], lhsT=wv_codes[j // 2][:, plane_cols].bitcast(FP8X4), lhsT_scale=wv_scale[j // 2][:, plane_cols],
+                rhs=emb_codes[:, first:stop].bitcast(FP8X4), rhs_scale=emb_scale[:, first:stop], start=True, stop=True,
             )
-            v_sb = sb.tile([P, I], F32, name="v_sb%d" % j, align_bytes=64)
+            v_sb = sb.tile([P, stop - first], F32, name="v_sb%d_%d" % (j, first), align_bytes=64)
             nc.scalar.copy(v_sb[:], v_ps[:])
-            nc.vector.tensor_copy(pages[j][:].indirect(offs2_sb[:]), v_sb[:])
+            nc.vector.tensor_copy(pages[j][:].indirect(offs2_sb[:, first // LIST_ROWS : stop // LIST_ROWS]), v_sb[:])
+
+        place_v(0, 0, I // 2, "bank0")
+        place_v(1, 0, I // 2, "bank1")
+        place_v(0, I // 2, I, "back0")
+        place_v(1, I // 2, I, "back1")
+        place_v(2, 0, I, "bank2")
+        place_v(3, 0, I, "bank3")
 
         wo_dealt = sb.tile([P, PACK, P, PACK], BF16, name="wo_dealt", align_bytes=64)
         deal(nc.scalar.copy, wo_dealt[:], wo_raw[:])
 
-        turned = []
+        turned = sb.tile([P, TURNED_PLANES, CHUNKS, P], BF16, name="turned", tag="wo_raw", align_bytes=64)
+        sum_ps = [ps.tile([P, CHUNKS, P], F32, name="sum_ps%d" % j) for j in range(TURNED_PLANES)]
         for j in range(TURNED_PLANES):
-            sum_ps = ps.tile([P, CHUNKS, P], F32, name="sum_ps%d" % j)
             for c in range(CHUNKS):
-                cols = chunk_cols(c, c + 1)
-                nc.tensor.matmul(sum_ps[:, c, :], lhsT=base_sb[0][:, j, cols], rhs=ident[:], is_transpose=True, start=True, stop=False)
-                nc.tensor.matmul(sum_ps[:, c, :], lhsT=pages[j][:, cols], rhs=ident[:], is_transpose=True, start=False, stop=True)
-            turned.append(sb.tile([P, CHUNKS, P], BF16, name="turned%d" % j, align_bytes=64))
-            nc.scalar.copy(turned[j][:], sum_ps[:])
+                nc.tensor.matmul(
+                    sum_ps[j][:, c, :], lhsT=base_sb[0][:, j, chunk_cols(c, c + 1)], rhs=ident[:],
+                    is_transpose=True, start=(c == 0), stop=False,
+                )
         for j in range(TURNED_PLANES):
-            back_ps = ps.tile([P, T], BF16, name="back_ps%d" % j)
             for c in range(CHUNKS):
-                nc.tensor.transpose(back_ps[:, chunk_cols(c, c + 1)], turned[j][:, c, :], ident_bf[:])
+                nc.tensor.matmul(
+                    sum_ps[j][:, c, :], lhsT=pages[j][:, chunk_cols(c, c + 1)], rhs=ident[:],
+                    is_transpose=True, start=False, stop=(c == LAST),
+                )
+            nc.scalar.copy(turned[:, j], sum_ps[j][:])
+        for j in range(TURNED_PLANES):
+            back_ps = ps.tile([P, T], BF16, name="back_ps%d" % j, tag="back%d" % j)
+            for c in range(CHUNKS):
+                nc.tensor.transpose(back_ps[:, chunk_cols(c, c + 1)], turned[:, j, c, :], ident_bf[:])
             nc.scalar.copy(x_planes[:, j, :], back_ps[:])
 
         wo_scale = sb.tile([P, F], U8, name="wo_scale", align_bytes=64)

@@ -66,8 +66,8 @@ def tile_attend_headpage_proj_pl_kernel(tc, emb_words, emb_scales, wv, base, wo,
         nc.sync.dma_start(words[:], emb_words[0].rearrange("p u r -> p (u r)").bitcast(I32))
         nc.sync.dma_start(offs2_sb[:], offs2)
         base_hbm = base.rearrange("(p j) t -> p j t", j=PACK)
-        nc.sync.dma_start(base_sb[0][:], base_hbm[:, 0:2, :])
         nc.sync.dma_start(wo_raw[:], wo.rearrange("(p j) f -> p j f", j=PACK))
+        nc.sync.dma_start(base_sb[0][:], base_hbm[:, 0:2, :])
         nc.sync.dma_start(base_sb[1][:], base_hbm[:, 2:4, :])
 
         wv_dealt = sb.tile([P, PACK, P, PACK], BF16, name="wv_dealt", align_bytes=64)
@@ -122,7 +122,7 @@ def tile_attend_headpage_proj_pl_kernel(tc, emb_words, emb_scales, wv, base, wo,
         deal(nc.scalar.copy, wo_dealt[:], wo_raw[:])
 
         turned = sb.tile([P, TURNED_PLANES, CHUNKS, P], BF16, name="turned", tag="wo_raw", align_bytes=64)
-        sum_ps = [ps.tile([P, CHUNKS, P], F32, name="sum_ps%d" % j) for j in range(TURNED_PLANES)]
+        sum_ps = [ps.tile([P, CHUNKS, P], F32, name="sum_ps%d" % j, tag="sum%d" % j) for j in range(TURNED_PLANES)]
         for j in range(TURNED_PLANES):
             for c in range(CHUNKS):
                 nc.tensor.matmul(
@@ -171,10 +171,14 @@ def tile_attend_headpage_proj_pl_kernel(tc, emb_words, emb_scales, wv, base, wo,
             nc.vector.quantize_mx(x_codes[c][:].bitcast(FP8X4), x_scale[c][:], x_woven[c][:].rearrange("p t j -> p (t j)"))
 
         def project(c):
-            y_ps[c] = ps.tile([P, PACK, CHUNK], F32, name="y_ps%d" % c, tag="bank%d" % c)
+            if c == 0:
+                y_ps[c] = [ps.tile([P, 2, CHUNK], F32, name="y_ps0_%d" % h, tag=("sum0", "bank0")[h]) for h in range(2)]
+            else:
+                y_ps[c] = [ps.tile([P, PACK, CHUNK], F32, name="y_ps%d" % c, tag="bank%d" % c)]
+            per_bank = PACK // len(y_ps[c])
             for s in range(PACK):
                 nc.tensor.matmul_mx(
-                    y_ps[c][:, s, :],
+                    y_ps[c][s // per_bank][:, s % per_bank, :],
                     lhsT=wo_codes[s // 2][:, P * (s % 2) : P * (s % 2 + 1)].bitcast(FP8X4),
                     lhsT_scale=wo_scale[:, P * s : P * (s + 1)],
                     rhs=x_codes[c][:].bitcast(FP8X4), rhs_scale=x_scale[c][:], start=True, stop=True,
@@ -182,8 +186,11 @@ def tile_attend_headpage_proj_pl_kernel(tc, emb_words, emb_scales, wv, base, wo,
 
         def hand_out(c):
             cols = chunk_cols(c, c + 1)
-            nc.scalar.copy(y_sb[:, :, cols], y_ps[c][:])
-            nc.sync.dma_start(y_hbm[:, :, cols], y_sb[:, :, cols])
+            per_bank = PACK // len(y_ps[c])
+            for h, bank in enumerate(y_ps[c]):
+                planes = slice(per_bank * h, per_bank * (h + 1))
+                nc.scalar.copy(y_sb[:, planes, cols], bank[:])
+                nc.sync.dma_start(y_hbm[:, planes, cols], y_sb[:, planes, cols])
             y_woven = sb.tile([P, CHUNK, PACK], BF16, name="y_woven%d" % c, align_bytes=64)
             weave(nc.vector.tensor_copy, y_woven[:], y_sb[:, :, cols])
             nc.vector.quantize_mx(y_codes[:, cols].bitcast(FP8X4), y_scale[:, cols], y_woven[:].rearrange("p t j -> p (t j)"))

@@ -60,8 +60,8 @@ def tile_attend_headpage_proj_pl_kernel(tc, emb_words, emb_scales, wv, base, wo,
 
         nc.vector.memset(scale_rows[:].bitcast(I32), 0)
         nc.sync.dma_start(wv_raw[:], wv.rearrange("(p j) e -> p j e", j=PACK))
-        for r in range(PACK):
-            nc.sync.dma_start(scale_rows[r:P:32, :].bitcast(I32), emb_scales[0, r : 16 : PACK, :].bitcast(I32))
+        for q in range(QUADRANTS):
+            nc.sync.dma_start(scale_rows[32 * q : 32 * q + 4, :].bitcast(I32), emb_scales[0, 4 * q : 4 * q + 4, :].bitcast(I32))
         nc.sync.dma_start(offs_sb[:], offs)
         nc.sync.dma_start(words[:], emb_words[0].rearrange("p u r -> p (u r)").bitcast(I32))
         nc.sync.dma_start(offs2_sb[:], offs2)
@@ -98,72 +98,68 @@ def tile_attend_headpage_proj_pl_kernel(tc, emb_words, emb_scales, wv, base, wo,
         make_identity(nc, ident[:])
         make_identity(nc, ident_bf[:])
 
-        x_planes = sb.tile([P, PACK, T], BF16, name="x_planes", align_bytes=64)
-
-        def place_v(j, first, stop, tag):
+        for j in range(PACK):
             plane_cols = slice(P * (j % 2), P * (j % 2 + 1))
-            v_ps = ps.tile([P, stop - first], F32, name="v_ps%d_%d" % (j, first), tag=tag)
+            v_ps = ps.tile([P, I], F32, name="v_ps%d" % j, tag="bank%d" % j)
             nc.tensor.matmul_mx(
                 v_ps[:], lhsT=wv_codes[j // 2][:, plane_cols].bitcast(FP8X4), lhsT_scale=wv_scale[j // 2][:, plane_cols],
-                rhs=emb_codes[:, first:stop].bitcast(FP8X4), rhs_scale=emb_scale[:, first:stop], start=True, stop=True,
+                rhs=emb_codes[:].bitcast(FP8X4), rhs_scale=emb_scale[:], start=True, stop=True,
             )
-            v_sb = sb.tile([P, stop - first], F32, name="v_sb%d_%d" % (j, first), align_bytes=64)
+            v_sb = sb.tile([P, I], F32, name="v_sb%d" % j, align_bytes=64)
             nc.scalar.copy(v_sb[:], v_ps[:])
-            nc.vector.tensor_copy(pages[j][:].indirect(offs2_sb[:, first // LIST_ROWS : stop // LIST_ROWS]), v_sb[:])
-
-        place_v(0, 0, I // 2, "bank0")
-        place_v(1, 0, I // 2, "bank1")
-        place_v(0, I // 2, I, "back0")
-        place_v(1, I // 2, I, "back1")
-        place_v(2, 0, I, "bank2")
-        place_v(3, 0, I, "bank3")
+            nc.vector.tensor_copy(pages[j][:].indirect(offs2_sb[:]), v_sb[:])
 
         wo_dealt = sb.tile([P, PACK, P, PACK], BF16, name="wo_dealt", align_bytes=64)
         deal(nc.scalar.copy, wo_dealt[:], wo_raw[:])
 
-        turned = sb.tile([P, TURNED_PLANES, CHUNKS, P], BF16, name="turned", tag="wo_raw", align_bytes=64)
-        sum_ps = [ps.tile([P, CHUNKS, P], F32, name="sum_ps%d" % j, tag="sum%d" % j) for j in range(TURNED_PLANES)]
-        for j in range(TURNED_PLANES):
-            for c in range(CHUNKS):
-                nc.tensor.matmul(
-                    sum_ps[j][:, c, :], lhsT=base_sb[0][:, j, chunk_cols(c, c + 1)], rhs=ident[:],
-                    is_transpose=True, start=(c == 0), stop=False,
-                )
-        for j in range(TURNED_PLANES):
-            for c in range(CHUNKS):
-                nc.tensor.matmul(
-                    sum_ps[j][:, c, :], lhsT=pages[j][:, chunk_cols(c, c + 1)], rhs=ident[:],
-                    is_transpose=True, start=False, stop=(c == LAST),
-                )
-            nc.scalar.copy(turned[:, j], sum_ps[j][:])
-        for j in range(TURNED_PLANES):
-            back_ps = ps.tile([P, T], BF16, name="back_ps%d" % j, tag="back%d" % j)
-            for c in range(CHUNKS):
-                nc.tensor.transpose(back_ps[:, chunk_cols(c, c + 1)], turned[:, j, c, :], ident_bf[:])
-            nc.scalar.copy(x_planes[:, j, :], back_ps[:])
+        x_half = [sb.tile([P, PACK, T // 2], BF16, name="x_half%d" % h, tag="x_half%d" % h, align_bytes=64) for h in range(2)]
 
+        def x_plane(j, first, stop):
+            h = first // 2
+            return x_half[h][:, j, chunk_cols(first - 2 * h, stop - 2 * h)]
+
+        def add_base(engine, j, first, stop):
+            cols = chunk_cols(first, stop)
+            engine.tensor_tensor(x_plane(j, first, stop), pages[j][:, cols], base_sb[j // 2][:, j % 2, cols], ADD)
+
+        add_base(nc.gpsimd, 0, 0, 2)
+        add_base(nc.gpsimd, 0, 2, 4)
+        add_base(nc.gpsimd, 2, 0, 2)
+
+        turned_parts = [(1, 0, CHUNKS), (2, 2, CHUNKS)]
+        turned = sb.tile([P, len(turned_parts), CHUNKS, P], BF16, name="turned", tag="wo_raw", align_bytes=64)
+        for n, (j, first, stop) in enumerate(turned_parts):
+            sum_ps = ps.tile([P, CHUNKS, P], F32, name="sum_ps%d" % n)
+            for c in range(first, stop):
+                nc.tensor.matmul(
+                    sum_ps[:, c, :], lhsT=base_sb[j // 2][:, j % 2, chunk_cols(c, c + 1)], rhs=ident[:],
+                    is_transpose=True, start=(c == first), stop=False,
+                )
+            for c in range(first, stop):
+                nc.tensor.matmul(
+                    sum_ps[:, c, :], lhsT=pages[j][:, chunk_cols(c, c + 1)], rhs=ident[:],
+                    is_transpose=True, start=False, stop=(c == stop - 1),
+                )
+            nc.scalar.copy(turned[:, n, first:stop], sum_ps[:, first:stop])
+        for n, (j, first, stop) in enumerate(turned_parts):
+            back_ps = ps.tile([P, T], BF16, name="back_ps%d" % n)
+            for c in range(first, stop):
+                nc.tensor.transpose(back_ps[:, chunk_cols(c, c + 1)], turned[:, n, c, :], ident_bf[:])
+            for c in range(first, stop, 2):
+                nc.scalar.copy(x_plane(j, c, c + 2), back_ps[:, chunk_cols(c, c + 2)])
+
+        wo_codes = sb.tile([P, F], U32, name="wo_codes", align_bytes=64)
         wo_scale = sb.tile([P, F], U8, name="wo_scale", align_bytes=64)
         y_sb = sb.tile([P, PACK, T], F32, name="y_sb", align_bytes=64)
         y_codes = sb.tile([P, T], U32, name="y_codes", align_bytes=64)
         y_scale = sb.tile([P, T], U8, name="y_scale", align_bytes=64)
         y_hbm = out_0.rearrange("(p s) t -> p s t", s=PACK)
         codes_hbm = out_1[0].rearrange("p t r -> p (t r)").bitcast(I32)
-        wo_codes, x_woven, x_codes, x_scale, y_ps = {}, {}, {}, {}, {}
-
-        def add_base(cols):
-            for j in range(TURNED_PLANES, PACK):
-                nc.vector.tensor_tensor(x_planes[:, j, cols], pages[j][:, cols], base_sb[1][:, j - TURNED_PLANES, cols], ADD)
-
-        def quantize_wo(h, reused_tag):
-            wo_codes[h] = sb.tile([P, F // 2], U32, name="wo_codes%d" % h, tag=reused_tag, align_bytes=64)
-            nc.vector.quantize_mx(
-                wo_codes[h][:].bitcast(FP8X4), wo_scale[:, F // 2 * h : F // 2 * (h + 1)],
-                wo_dealt[:, 2 * h : 2 * h + 2].rearrange("p s m j -> p (s m j)"),
-            )
+        x_woven, x_codes, x_scale, y_ps = {}, {}, {}, {}
 
         def weave_x(c, engine_copy, tag):
             x_woven[c] = sb.tile([P, CHUNK, PACK], BF16, name="x_woven%d" % c, tag=tag, align_bytes=64)
-            weave(engine_copy, x_woven[c][:], x_planes[:, :, chunk_cols(c, c + 1)])
+            weave(engine_copy, x_woven[c][:], x_half[c // 2][:, :, chunk_cols(c % 2, c % 2 + 1)])
 
         def quantize_x(c):
             x_codes[c] = sb.tile([P, CHUNK], U32, name="x_codes%d" % c, align_bytes=64)
@@ -171,41 +167,33 @@ def tile_attend_headpage_proj_pl_kernel(tc, emb_words, emb_scales, wv, base, wo,
             nc.vector.quantize_mx(x_codes[c][:].bitcast(FP8X4), x_scale[c][:], x_woven[c][:].rearrange("p t j -> p (t j)"))
 
         def project(c):
-            if c == 0:
-                y_ps[c] = [ps.tile([P, 2, CHUNK], F32, name="y_ps0_%d" % h, tag=("sum0", "bank0")[h]) for h in range(2)]
-            else:
-                y_ps[c] = [ps.tile([P, PACK, CHUNK], F32, name="y_ps%d" % c, tag="bank%d" % c)]
-            per_bank = PACK // len(y_ps[c])
+            y_ps[c] = ps.tile([P, PACK, CHUNK], F32, name="y_ps%d" % c, tag="bank%d" % c)
             for s in range(PACK):
                 nc.tensor.matmul_mx(
-                    y_ps[c][s // per_bank][:, s % per_bank, :],
-                    lhsT=wo_codes[s // 2][:, P * (s % 2) : P * (s % 2 + 1)].bitcast(FP8X4),
+                    y_ps[c][:, s, :],
+                    lhsT=wo_codes[:, P * s : P * (s + 1)].bitcast(FP8X4),
                     lhsT_scale=wo_scale[:, P * s : P * (s + 1)],
                     rhs=x_codes[c][:].bitcast(FP8X4), rhs_scale=x_scale[c][:], start=True, stop=True,
                 )
 
         def hand_out(c):
             cols = chunk_cols(c, c + 1)
-            per_bank = PACK // len(y_ps[c])
-            for h, bank in enumerate(y_ps[c]):
-                planes = slice(per_bank * h, per_bank * (h + 1))
-                nc.scalar.copy(y_sb[:, planes, cols], bank[:])
-                nc.sync.dma_start(y_hbm[:, planes, cols], y_sb[:, planes, cols])
+            nc.scalar.copy(y_sb[:, :, cols], y_ps[c][:])
+            nc.sync.dma_start(y_hbm[:, :, cols], y_sb[:, :, cols])
             y_woven = sb.tile([P, CHUNK, PACK], BF16, name="y_woven%d" % c, align_bytes=64)
             weave(nc.vector.tensor_copy, y_woven[:], y_sb[:, :, cols])
             nc.vector.quantize_mx(y_codes[:, cols].bitcast(FP8X4), y_scale[:, cols], y_woven[:].rearrange("p t j -> p (t j)"))
 
-        add_base(chunk_cols(0, 1))
-        add_base(chunk_cols(1, 2))
-        add_base(chunk_cols(2, CHUNKS))
-        quantize_wo(0, "page2")
+        add_base(nc.vector, 3, 0, 1)
+        add_base(nc.vector, 3, 1, 2)
+        add_base(nc.vector, 3, 2, 4)
+        nc.vector.quantize_mx(wo_codes[:].bitcast(FP8X4), wo_scale[:], wo_dealt[:].rearrange("p s m j -> p (s m j)"))
         for c in range(LAST):
             weave_x(c, nc.scalar.copy, "x_woven%d" % c)
         quantize_x(0)
-        quantize_wo(1, "x_woven0")
-        for c in range(1, LAST):
-            quantize_x(c)
-        weave_x(LAST, nc.vector.tensor_copy, "x_woven1")
+        quantize_x(1)
+        weave_x(LAST, nc.vector.tensor_copy, "x_half0")
+        quantize_x(2)
         quantize_x(LAST)
         for c in range(CHUNKS):
             project(c)

@@ -60,8 +60,8 @@ def tile_attend_headpage_proj_pl_kernel(tc, emb_words, emb_scales, wv, base, wo,
 
         nc.vector.memset(scale_rows[:].bitcast(I32), 0)
         nc.sync.dma_start(wv_raw[:], wv.rearrange("(p j) e -> p j e", j=PACK))
-        for q in range(QUADRANTS):
-            nc.sync.dma_start(scale_rows[32 * q : 32 * q + 4, :].bitcast(I32), emb_scales[0, 4 * q : 4 * q + 4, :].bitcast(I32))
+        for r in range(PACK):
+            nc.sync.dma_start(scale_rows[r:P:32, :].bitcast(I32), emb_scales[0, r : 16 : PACK, :].bitcast(I32))
         nc.sync.dma_start(offs_sb[:], offs)
         nc.sync.dma_start(words[:], emb_words[0].rearrange("p u r -> p (u r)").bitcast(I32))
         nc.sync.dma_start(offs2_sb[:], offs2)
@@ -112,29 +112,28 @@ def tile_attend_headpage_proj_pl_kernel(tc, emb_words, emb_scales, wv, base, wo,
         wo_dealt = sb.tile([P, PACK, P, PACK], BF16, name="wo_dealt", align_bytes=64)
         deal(nc.scalar.copy, wo_dealt[:], wo_raw[:])
 
-        x_half = [sb.tile([P, PACK, T // 2], BF16, name="x_half%d" % h, tag="x_half%d" % h, align_bytes=64) for h in range(2)]
+        x_first = sb.tile([P, PACK, CHUNK], BF16, name="x_first", tag="x_first", align_bytes=64)
+        x_rest = sb.tile([P, PACK, T - CHUNK], BF16, name="x_rest", align_bytes=64)
 
         def x_plane(j, first, stop):
-            h = first // 2
-            return x_half[h][:, j, chunk_cols(first - 2 * h, stop - 2 * h)]
+            return x_first[:, j, :] if first == 0 else x_rest[:, j, chunk_cols(first - 1, stop - 1)]
 
         def add_base(engine, j, first, stop):
             cols = chunk_cols(first, stop)
             engine.tensor_tensor(x_plane(j, first, stop), pages[j][:, cols], base_sb[j // 2][:, j % 2, cols], ADD)
 
-        add_base(nc.gpsimd, 0, 0, 2)
-        add_base(nc.gpsimd, 0, 2, 4)
-        add_base(nc.gpsimd, 2, 0, 2)
-
-        turned_parts = [(1, 0, CHUNKS), (2, 2, CHUNKS)]
+        turned_parts = [(0, 0, CHUNKS), (1, 0, CHUNKS)]
         turned = sb.tile([P, len(turned_parts), CHUNKS, P], BF16, name="turned", tag="wo_raw", align_bytes=64)
+        sums = [ps.tile([P, CHUNKS, P], F32, name="sum_ps%d" % n) for n in range(2)]
         for n, (j, first, stop) in enumerate(turned_parts):
-            sum_ps = ps.tile([P, CHUNKS, P], F32, name="sum_ps%d" % n)
+            sum_ps = sums[n]
             for c in range(first, stop):
                 nc.tensor.matmul(
                     sum_ps[:, c, :], lhsT=base_sb[j // 2][:, j % 2, chunk_cols(c, c + 1)], rhs=ident[:],
                     is_transpose=True, start=(c == first), stop=False,
                 )
+        for n, (j, first, stop) in enumerate(turned_parts):
+            sum_ps = sums[n]
             for c in range(first, stop):
                 nc.tensor.matmul(
                     sum_ps[:, c, :], lhsT=pages[j][:, chunk_cols(c, c + 1)], rhs=ident[:],
@@ -145,21 +144,29 @@ def tile_attend_headpage_proj_pl_kernel(tc, emb_words, emb_scales, wv, base, wo,
             back_ps = ps.tile([P, T], BF16, name="back_ps%d" % n)
             for c in range(first, stop):
                 nc.tensor.transpose(back_ps[:, chunk_cols(c, c + 1)], turned[:, n, c, :], ident_bf[:])
-            for c in range(first, stop, 2):
-                nc.scalar.copy(x_plane(j, c, c + 2), back_ps[:, chunk_cols(c, c + 2)])
+            nc.scalar.copy(x_plane(j, 0, 1), back_ps[:, chunk_cols(0, 1)])
+            nc.scalar.copy(x_plane(j, 1, CHUNKS), back_ps[:, chunk_cols(1, CHUNKS)])
 
-        wo_codes = sb.tile([P, F], U32, name="wo_codes", align_bytes=64)
+        wo_codes = {}
         wo_scale = sb.tile([P, F], U8, name="wo_scale", align_bytes=64)
         y_sb = sb.tile([P, PACK, T], F32, name="y_sb", align_bytes=64)
+        y_woven = sb.tile([P, T, PACK], BF16, name="y_woven", align_bytes=64)
         y_codes = sb.tile([P, T], U32, name="y_codes", align_bytes=64)
         y_scale = sb.tile([P, T], U8, name="y_scale", align_bytes=64)
         y_hbm = out_0.rearrange("(p s) t -> p s t", s=PACK)
         codes_hbm = out_1[0].rearrange("p t r -> p (t r)").bitcast(I32)
         x_woven, x_codes, x_scale, y_ps = {}, {}, {}, {}
 
+        def quantize_wo(h, reused_tag):
+            wo_codes[h] = sb.tile([P, F // 2], U32, name="wo_codes%d" % h, tag=reused_tag, align_bytes=64)
+            nc.vector.quantize_mx(
+                wo_codes[h][:].bitcast(FP8X4), wo_scale[:, F // 2 * h : F // 2 * (h + 1)],
+                wo_dealt[:, 2 * h : 2 * h + 2].rearrange("p s m j -> p (s m j)"),
+            )
+
         def weave_x(c, engine_copy, tag):
             x_woven[c] = sb.tile([P, CHUNK, PACK], BF16, name="x_woven%d" % c, tag=tag, align_bytes=64)
-            weave(engine_copy, x_woven[c][:], x_half[c // 2][:, :, chunk_cols(c % 2, c % 2 + 1)])
+            weave(engine_copy, x_woven[c][:], x_plane(slice(0, PACK), c, c + 1))
 
         def quantize_x(c):
             x_codes[c] = sb.tile([P, CHUNK], U32, name="x_codes%d" % c, align_bytes=64)
@@ -171,7 +178,7 @@ def tile_attend_headpage_proj_pl_kernel(tc, emb_words, emb_scales, wv, base, wo,
             for s in range(PACK):
                 nc.tensor.matmul_mx(
                     y_ps[c][:, s, :],
-                    lhsT=wo_codes[:, P * s : P * (s + 1)].bitcast(FP8X4),
+                    lhsT=wo_codes[s // 2][:, P * (s % 2) : P * (s % 2 + 1)].bitcast(FP8X4),
                     lhsT_scale=wo_scale[:, P * s : P * (s + 1)],
                     rhs=x_codes[c][:].bitcast(FP8X4), rhs_scale=x_scale[c][:], start=True, stop=True,
                 )
@@ -180,29 +187,34 @@ def tile_attend_headpage_proj_pl_kernel(tc, emb_words, emb_scales, wv, base, wo,
             cols = chunk_cols(c, c + 1)
             nc.scalar.copy(y_sb[:, :, cols], y_ps[c][:])
             nc.sync.dma_start(y_hbm[:, :, cols], y_sb[:, :, cols])
-            y_woven = sb.tile([P, CHUNK, PACK], BF16, name="y_woven%d" % c, align_bytes=64)
-            weave(nc.vector.tensor_copy, y_woven[:], y_sb[:, :, cols])
-            nc.vector.quantize_mx(y_codes[:, cols].bitcast(FP8X4), y_scale[:, cols], y_woven[:].rearrange("p t j -> p (t j)"))
+            weave(nc.vector.tensor_copy, y_woven[:, cols], y_sb[:, :, cols])
 
-        add_base(nc.vector, 3, 0, 1)
-        add_base(nc.vector, 3, 1, 2)
-        add_base(nc.vector, 3, 2, 4)
-        nc.vector.quantize_mx(wo_codes[:].bitcast(FP8X4), wo_scale[:], wo_dealt[:].rearrange("p s m j -> p (s m j)"))
+        def quantize_y(first, stop):
+            cols = chunk_cols(first, stop)
+            nc.vector.quantize_mx(y_codes[:, cols].bitcast(FP8X4), y_scale[:, cols], y_woven[:, cols].rearrange("p t j -> p (t j)"))
+
+        for first, stop in ((0, 1), (1, 2), (2, 4)):
+            add_base(nc.vector, 2, first, stop)
+            add_base(nc.vector, 3, first, stop)
+        quantize_wo(0, "page2")
         for c in range(LAST):
             weave_x(c, nc.scalar.copy, "x_woven%d" % c)
         quantize_x(0)
+        quantize_wo(1, "x_first")
         quantize_x(1)
-        weave_x(LAST, nc.vector.tensor_copy, "x_half0")
         quantize_x(2)
+        weave_x(LAST, nc.vector.tensor_copy, "x_woven1")
         quantize_x(LAST)
         for c in range(CHUNKS):
             project(c)
 
         for c in range(LAST):
             hand_out(c)
+            quantize_y(c, c + 1)
         early, late = chunk_cols(0, LAST), chunk_cols(LAST, CHUNKS)
         nc.sync.dma_start(codes_hbm[:, early], y_codes[:, early].bitcast(I32))
         hand_out(LAST)
+        quantize_y(LAST, CHUNKS)
         nc.scalar.dma_start(codes_hbm[:, late], y_codes[:, late].bitcast(I32))
         for q in range(QUADRANTS):
             queue = nc.scalar if q % 2 else nc.sync

@@ -100,13 +100,18 @@ def tile_attend_headpage_proj_pl_kernel(tc, emb_words, emb_scales, wv, base, wo,
 
         for j in range(PACK):
             plane_cols = slice(P * (j % 2), P * (j % 2 + 1))
-            v_ps = ps.tile([P, I], F32, name="v_ps%d" % j, tag="bank%d" % j)
-            nc.tensor.matmul_mx(
-                v_ps[:], lhsT=wv_codes[j // 2][:, plane_cols].bitcast(FP8X4), lhsT_scale=wv_scale[j // 2][:, plane_cols],
-                rhs=emb_codes[:].bitcast(FP8X4), rhs_scale=emb_scale[:], start=True, stop=True,
-            )
             v_sb = sb.tile([P, I], F32, name="v_sb%d" % j, align_bytes=64)
-            nc.scalar.copy(v_sb[:], v_ps[:])
+            if j == 0:
+                parts = [(slice(0, I // 2), "bank0", nc.scalar.copy), (slice(I // 2, I), "back0", nc.vector.tensor_copy)]
+            else:
+                parts = [(slice(0, I), "bank%d" % j, nc.scalar.copy)]
+            for slots, tag, engine_copy in parts:
+                v_ps = ps.tile([P, slots.stop - slots.start], F32, name="v_ps%d_%d" % (j, slots.start), tag=tag)
+                nc.tensor.matmul_mx(
+                    v_ps[:], lhsT=wv_codes[j // 2][:, plane_cols].bitcast(FP8X4), lhsT_scale=wv_scale[j // 2][:, plane_cols],
+                    rhs=emb_codes[:, slots].bitcast(FP8X4), rhs_scale=emb_scale[:, slots], start=True, stop=True,
+                )
+                engine_copy(v_sb[:, slots], v_ps[:])
             nc.vector.tensor_copy(pages[j][:].indirect(offs2_sb[:]), v_sb[:])
 
         wo_dealt = sb.tile([P, PACK, P, PACK], BF16, name="wo_dealt", align_bytes=64)
@@ -141,7 +146,7 @@ def tile_attend_headpage_proj_pl_kernel(tc, emb_words, emb_scales, wv, base, wo,
                 )
             nc.scalar.copy(turned[:, n, first:stop], sum_ps[:, first:stop])
         for n, (j, first, stop) in enumerate(turned_parts):
-            back_ps = ps.tile([P, T], BF16, name="back_ps%d" % n)
+            back_ps = ps.tile([P, T], BF16, name="back_ps%d" % n, tag="back%d" % n)
             for c in range(first, stop):
                 nc.tensor.transpose(back_ps[:, chunk_cols(c, c + 1)], turned[:, n, c, :], ident_bf[:])
             nc.scalar.copy(x_plane(j, 0, 1), back_ps[:, chunk_cols(0, 1)])
@@ -208,13 +213,15 @@ def tile_attend_headpage_proj_pl_kernel(tc, emb_words, emb_scales, wv, base, wo,
         for c in range(CHUNKS):
             project(c)
 
-        for c in range(LAST):
-            hand_out(c)
-            quantize_y(c, c + 1)
-        early, late = chunk_cols(0, LAST), chunk_cols(LAST, CHUNKS)
+        hand_out(0)
+        hand_out(1)
+        quantize_y(0, 2)
+        early, late = chunk_cols(0, 2), chunk_cols(2, CHUNKS)
         nc.sync.dma_start(codes_hbm[:, early], y_codes[:, early].bitcast(I32))
-        hand_out(LAST)
-        quantize_y(LAST, CHUNKS)
+        hand_out(2)
+        hand_out(3)
+        quantize_y(2, 3)
+        quantize_y(3, 4)
         nc.scalar.dma_start(codes_hbm[:, late], y_codes[:, late].bitcast(I32))
         for q in range(QUADRANTS):
             queue = nc.scalar if q % 2 else nc.sync

@@ -129,7 +129,7 @@ def tile_attend_headpage_proj_pl_kernel(tc, emb_words, emb_scales, wv, base, wo,
 
         turned_parts = [(0, 0, CHUNKS), (1, 0, CHUNKS)]
         turned = sb.tile([P, len(turned_parts), CHUNKS, P], BF16, name="turned", tag="wo_raw", align_bytes=64)
-        sums = [ps.tile([P, CHUNKS, P], F32, name="sum_ps%d" % n) for n in range(2)]
+        sums = [ps.tile([P, CHUNKS, P], F32, name="sum_ps%d" % n, tag="sum%d" % n) for n in range(2)]
         for n, (j, first, stop) in enumerate(turned_parts):
             sum_ps = sums[n]
             for c in range(first, stop):
@@ -161,6 +161,7 @@ def tile_attend_headpage_proj_pl_kernel(tc, emb_words, emb_scales, wv, base, wo,
         y_hbm = out_0.rearrange("(p s) t -> p s t", s=PACK)
         codes_hbm = out_1[0].rearrange("p t r -> p (t r)").bitcast(I32)
         x_woven, x_codes, x_scale, y_ps = {}, {}, {}, {}
+        y_banks = ["bank0", "bank1", "bank2", "bank3", "sum0", "sum1", "back0", "back1"]
 
         def quantize_wo(h, reused_tag):
             wo_codes[h] = sb.tile([P, F // 2], U32, name="wo_codes%d" % h, tag=reused_tag, align_bytes=64)
@@ -179,10 +180,11 @@ def tile_attend_headpage_proj_pl_kernel(tc, emb_words, emb_scales, wv, base, wo,
             nc.vector.quantize_mx(x_codes[c][:].bitcast(FP8X4), x_scale[c][:], x_woven[c][:].rearrange("p t j -> p (t j)"))
 
         def project(c):
-            y_ps[c] = ps.tile([P, PACK, CHUNK], F32, name="y_ps%d" % c, tag="bank%d" % c)
             for s in range(PACK):
+                if s % 2 == 0:
+                    y_ps[c, s // 2] = ps.tile([P, 2, CHUNK], F32, name="y_ps%d_%d" % (c, s // 2), tag=y_banks[2 * c + s // 2])
                 nc.tensor.matmul_mx(
-                    y_ps[c][:, s, :],
+                    y_ps[c, s // 2][:, s % 2, :],
                     lhsT=wo_codes[s // 2][:, P * (s % 2) : P * (s % 2 + 1)].bitcast(FP8X4),
                     lhsT_scale=wo_scale[:, P * s : P * (s + 1)],
                     rhs=x_codes[c][:].bitcast(FP8X4), rhs_scale=x_scale[c][:], start=True, stop=True,
@@ -190,7 +192,8 @@ def tile_attend_headpage_proj_pl_kernel(tc, emb_words, emb_scales, wv, base, wo,
 
         def hand_out(c):
             cols = chunk_cols(c, c + 1)
-            nc.scalar.copy(y_sb[:, :, cols], y_ps[c][:])
+            for h in range(2):
+                nc.scalar.copy(y_sb[:, 2 * h : 2 * h + 2, cols], y_ps[c, h][:])
             nc.sync.dma_start(y_hbm[:, :, cols], y_sb[:, :, cols])
             weave(nc.vector.tensor_copy, y_woven[:, cols], y_sb[:, :, cols])
 

@@ -102,7 +102,7 @@ def tile_attend_headpage_proj_pl_kernel(tc, emb_words, emb_scales, wv, base, wo,
             plane_cols = slice(P * (j % 2), P * (j % 2 + 1))
             v_sb = sb.tile([P, I], F32, name="v_sb%d" % j, align_bytes=64)
             if j == 0:
-                parts = [(slice(0, I // 2), "bank0", nc.scalar.copy), (slice(I // 2, I), "back0", nc.vector.tensor_copy)]
+                parts = [(slice(0, I // 2), "bank0", nc.scalar.copy), (slice(I // 2, I), "back0", nc.scalar.copy)]
             else:
                 parts = [(slice(0, I), "bank%d" % j, nc.scalar.copy)]
             for slots, tag, engine_copy in parts:

@@ -24,6 +24,7 @@ CHUNKS = T // CHUNK
 LAST = CHUNKS - 1
 TURNED_PLANES = 2
 VECTOR_SHARE = 88
+EARLY_CHUNKS = 2
 
 
 def deal(engine_copy, dealt, raw):
@@ -102,16 +103,16 @@ def tile_attend_headpage_proj_pl_kernel(tc, emb_words, emb_scales, wv, base, wo,
             plane_cols = slice(P * (j % 2), P * (j % 2 + 1))
             v_sb = sb.tile([P, I], F32, name="v_sb%d" % j, align_bytes=64)
             if j == 0:
-                parts = [(slice(0, I // 2), "bank0", nc.scalar.copy), (slice(I // 2, I), "back0", nc.scalar.copy)]
+                parts = [(slice(0, I // 2), "bank0"), (slice(I // 2, I), "back0")]
             else:
-                parts = [(slice(0, I), "bank%d" % j, nc.scalar.copy)]
-            for slots, tag, engine_copy in parts:
+                parts = [(slice(0, I), "bank%d" % j)]
+            for slots, tag in parts:
                 v_ps = ps.tile([P, slots.stop - slots.start], F32, name="v_ps%d_%d" % (j, slots.start), tag=tag)
                 nc.tensor.matmul_mx(
                     v_ps[:], lhsT=wv_codes[j // 2][:, plane_cols].bitcast(FP8X4), lhsT_scale=wv_scale[j // 2][:, plane_cols],
                     rhs=emb_codes[:, slots].bitcast(FP8X4), rhs_scale=emb_scale[:, slots], start=True, stop=True,
                 )
-                engine_copy(v_sb[:, slots], v_ps[:])
+                nc.scalar.copy(v_sb[:, slots], v_ps[:])
             nc.vector.tensor_copy(pages[j][:].indirect(offs2_sb[:]), v_sb[:])
 
         wo_dealt = sb.tile([P, PACK, P, PACK], BF16, name="wo_dealt", align_bytes=64)
@@ -123,32 +124,29 @@ def tile_attend_headpage_proj_pl_kernel(tc, emb_words, emb_scales, wv, base, wo,
         def x_plane(j, first, stop):
             return x_first[:, j, :] if first == 0 else x_rest[:, j, chunk_cols(first - 1, stop - 1)]
 
-        def add_base(engine, j, first, stop):
+        def add_base(j, first, stop):
             cols = chunk_cols(first, stop)
-            engine.tensor_tensor(x_plane(j, first, stop), pages[j][:, cols], base_sb[j // 2][:, j % 2, cols], ADD)
+            nc.vector.tensor_tensor(x_plane(j, first, stop), pages[j][:, cols], base_sb[j // 2][:, j % 2, cols], ADD)
 
-        turned_parts = [(0, 0, CHUNKS), (1, 0, CHUNKS)]
-        turned = sb.tile([P, len(turned_parts), CHUNKS, P], BF16, name="turned", tag="wo_raw", align_bytes=64)
-        sums = [ps.tile([P, CHUNKS, P], F32, name="sum_ps%d" % n, tag="sum%d" % n) for n in range(2)]
-        for n, (j, first, stop) in enumerate(turned_parts):
-            sum_ps = sums[n]
-            for c in range(first, stop):
+        turned = sb.tile([P, TURNED_PLANES, CHUNKS, P], BF16, name="turned", tag="wo_raw", align_bytes=64)
+        sums = [ps.tile([P, CHUNKS, P], F32, name="sum_ps%d" % j, tag="sum%d" % j) for j in range(TURNED_PLANES)]
+        for j in range(TURNED_PLANES):
+            for c in range(CHUNKS):
                 nc.tensor.matmul(
-                    sum_ps[:, c, :], lhsT=base_sb[j // 2][:, j % 2, chunk_cols(c, c + 1)], rhs=ident[:],
-                    is_transpose=True, start=(c == first), stop=False,
+                    sums[j][:, c, :], lhsT=base_sb[j // 2][:, j % 2, chunk_cols(c, c + 1)], rhs=ident[:],
+                    is_transpose=True, start=(c == 0), stop=False,
                 )
-        for n, (j, first, stop) in enumerate(turned_parts):
-            sum_ps = sums[n]
-            for c in range(first, stop):
+        for j in range(TURNED_PLANES):
+            for c in range(CHUNKS):
                 nc.tensor.matmul(
-                    sum_ps[:, c, :], lhsT=pages[j][:, chunk_cols(c, c + 1)], rhs=ident[:],
-                    is_transpose=True, start=False, stop=(c == stop - 1),
+                    sums[j][:, c, :], lhsT=pages[j][:, chunk_cols(c, c + 1)], rhs=ident[:],
+                    is_transpose=True, start=False, stop=(c == LAST),
                 )
-            nc.scalar.copy(turned[:, n, first:stop], sum_ps[:, first:stop])
-        for n, (j, first, stop) in enumerate(turned_parts):
-            back_ps = ps.tile([P, T], BF16, name="back_ps%d" % n, tag="back%d" % n)
-            for c in range(first, stop):
-                nc.tensor.transpose(back_ps[:, chunk_cols(c, c + 1)], turned[:, n, c, :], ident_bf[:])
+            nc.scalar.copy(turned[:, j], sums[j][:])
+        for j in range(TURNED_PLANES):
+            back_ps = ps.tile([P, T], BF16, name="back_ps%d" % j, tag="back%d" % j)
+            for c in range(CHUNKS):
+                nc.tensor.transpose(back_ps[:, chunk_cols(c, c + 1)], turned[:, j, c, :], ident_bf[:])
             nc.scalar.copy(x_plane(j, 0, 1), back_ps[:, chunk_cols(0, 1)])
             nc.scalar.copy(x_plane(j, 1, CHUNKS), back_ps[:, chunk_cols(1, CHUNKS)])
 
@@ -201,9 +199,11 @@ def tile_attend_headpage_proj_pl_kernel(tc, emb_words, emb_scales, wv, base, wo,
             cols = chunk_cols(first, stop)
             nc.vector.quantize_mx(y_codes[:, cols].bitcast(FP8X4), y_scale[:, cols], y_woven[:, cols].rearrange("p t j -> p (t j)"))
 
-        for first, stop in ((0, 1), (1, 2), (2, 4)):
-            add_base(nc.vector, 2, first, stop)
-            add_base(nc.vector, 3, first, stop)
+        for j in range(TURNED_PLANES, PACK):
+            for c in range(2):
+                add_base(j, c, c + 1)
+        for j in range(TURNED_PLANES, PACK):
+            add_base(j, 2, CHUNKS)
         quantize_wo(0, "page2")
         for c in range(LAST):
             weave_x(c, nc.scalar.copy, "x_woven%d" % c)
@@ -216,15 +216,15 @@ def tile_attend_headpage_proj_pl_kernel(tc, emb_words, emb_scales, wv, base, wo,
         for c in range(CHUNKS):
             project(c)
 
-        hand_out(0)
-        hand_out(1)
-        quantize_y(0, 2)
-        early, late = chunk_cols(0, 2), chunk_cols(2, CHUNKS)
+        for c in range(EARLY_CHUNKS):
+            hand_out(c)
+        quantize_y(0, EARLY_CHUNKS)
+        early, late = chunk_cols(0, EARLY_CHUNKS), chunk_cols(EARLY_CHUNKS, CHUNKS)
         nc.sync.dma_start(codes_hbm[:, early], y_codes[:, early].bitcast(I32))
-        hand_out(2)
-        hand_out(3)
-        quantize_y(2, 3)
-        quantize_y(3, 4)
+        for c in range(EARLY_CHUNKS, CHUNKS):
+            hand_out(c)
+        for c in range(EARLY_CHUNKS, CHUNKS):
+            quantize_y(c, c + 1)
         nc.scalar.dma_start(codes_hbm[:, late], y_codes[:, late].bitcast(I32))
         for q in range(QUADRANTS):
             queue = nc.scalar if q % 2 else nc.sync

@@ -45,6 +45,10 @@ def chunk_cols(first, stop):
     return slice(CHUNK * first, CHUNK * stop)
 
 
+def list_cols(slots):
+    return slice(slots.start // LIST_ROWS, slots.stop // LIST_ROWS)
+
+
 def tile_attend_headpage_proj_pl_kernel(tc, emb_words, emb_scales, wv, base, wo, offs, offs2, out_0, out_1, out_2):
     nc = tc.nc
     with ExitStack() as ctx:
@@ -86,8 +90,10 @@ def tile_attend_headpage_proj_pl_kernel(tc, emb_words, emb_scales, wv, base, wo,
             )
 
         quantize_wv(0, "wv_codes0")
-        emb_codes = sb.tile([P, I], U32, name="emb_codes", align_bytes=64)
-        nc.vector.tensor_copy(emb_codes[:], words[:].bitcast(U32).indirect(offs_sb[:]))
+        emb_codes = sb.tile([P, I], U32, name="emb_codes", tag="emb_codes", align_bytes=64)
+        first_half, second_half, whole = slice(0, I // 2), slice(I // 2, I), slice(0, I)
+        for slots in (first_half, second_half):
+            nc.vector.tensor_copy(emb_codes[:, slots], words[:].bitcast(U32).indirect(offs_sb[:, list_cols(slots)]))
         quantize_wv(1, "words")
 
         pages = [sb.tile([P, T], F32, name="page%d" % j, tag="page%d" % j, align_bytes=64) for j in range(PACK)]
@@ -95,26 +101,23 @@ def tile_attend_headpage_proj_pl_kernel(tc, emb_words, emb_scales, wv, base, wo,
             nc.vector.memset(pages[j][:], 0.0)
 
         ident = sb.tile([P, P], F32, name="ident", align_bytes=64)
-        ident_bf = sb.tile([P, P], BF16, name="ident_bf", align_bytes=64)
         make_identity(nc, ident[:])
-        make_identity(nc, ident_bf[:])
 
-        for j in range(PACK):
+        pieces = [(0, first_half, "bank0"), (1, whole, "bank1"), (0, second_half, "back0"), (2, whole, "bank2"), (3, whole, "bank3")]
+        for n, (j, slots, tag) in enumerate(pieces):
             plane_cols = slice(P * (j % 2), P * (j % 2 + 1))
-            v_sb = sb.tile([P, I], F32, name="v_sb%d" % j, align_bytes=64)
-            if j == 0:
-                parts = [(slice(0, I // 2), "bank0"), (slice(I // 2, I), "back0")]
-            else:
-                parts = [(slice(0, I), "bank%d" % j)]
-            for slots, tag in parts:
-                v_ps = ps.tile([P, slots.stop - slots.start], F32, name="v_ps%d_%d" % (j, slots.start), tag=tag)
-                nc.tensor.matmul_mx(
-                    v_ps[:], lhsT=wv_codes[j // 2][:, plane_cols].bitcast(FP8X4), lhsT_scale=wv_scale[j // 2][:, plane_cols],
-                    rhs=emb_codes[:, slots].bitcast(FP8X4), rhs_scale=emb_scale[:, slots], start=True, stop=True,
-                )
-                nc.scalar.copy(v_sb[:, slots], v_ps[:])
-            nc.vector.tensor_copy(pages[j][:].indirect(offs2_sb[:]), v_sb[:])
+            width = slots.stop - slots.start
+            v_sb = sb.tile([P, width], F32, name="v_sb%d" % n, align_bytes=64)
+            v_ps = ps.tile([P, width], F32, name="v_ps%d" % n, tag=tag)
+            nc.tensor.matmul_mx(
+                v_ps[:], lhsT=wv_codes[j // 2][:, plane_cols].bitcast(FP8X4), lhsT_scale=wv_scale[j // 2][:, plane_cols],
+                rhs=emb_codes[:, slots].bitcast(FP8X4), rhs_scale=emb_scale[:, slots], start=True, stop=True,
+            )
+            nc.scalar.copy(v_sb[:], v_ps[:])
+            nc.vector.tensor_copy(pages[j][:].indirect(offs2_sb[:, list_cols(slots)]), v_sb[:])
 
+        ident_bf = sb.tile([P, P], BF16, name="ident_bf", tag="emb_codes", align_bytes=64)
+        nc.scalar.copy(ident_bf[:], ident[:])
         wo_dealt = sb.tile([P, PACK, P, PACK], BF16, name="wo_dealt", align_bytes=64)
         deal(nc.scalar.copy, wo_dealt[:], wo_raw[:])
 
@@ -136,14 +139,14 @@ def tile_attend_headpage_proj_pl_kernel(tc, emb_words, emb_scales, wv, base, wo,
                     sums[j][:, c, :], lhsT=base_sb[j // 2][:, j % 2, chunk_cols(c, c + 1)], rhs=ident[:],
                     is_transpose=True, start=(c == 0), stop=False,
                 )
-        for j in range(TURNED_PLANES):
+        for j in (1, 0):
             for c in range(CHUNKS):
                 nc.tensor.matmul(
                     sums[j][:, c, :], lhsT=pages[j][:, chunk_cols(c, c + 1)], rhs=ident[:],
                     is_transpose=True, start=False, stop=(c == LAST),
                 )
             nc.scalar.copy(turned[:, j], sums[j][:])
-        for j in range(TURNED_PLANES):
+        for j in (1, 0):
             back_ps = ps.tile([P, T], BF16, name="back_ps%d" % j, tag="back%d" % j)
             for c in range(CHUNKS):
                 nc.tensor.transpose(back_ps[:, chunk_cols(c, c + 1)], turned[:, j, c, :], ident_bf[:])

@@ -80,21 +80,13 @@ def tile_attend_headpage_proj_pl_kernel(tc, emb_words, emb_scales, wv, base, wo,
         deal(nc.scalar.copy, wv_dealt[:, :, VECTOR_SHARE:, :], wv_raw[:, :, PACK * VECTOR_SHARE :])
         emb_scale = sb.tile([P, I], U8, name="emb_scale", align_bytes=64)
         nc.vector.tensor_copy(emb_scale[:], scale_rows[:].indirect(offs_sb[:]))
-        wv_codes, wv_scale = {}, {}
-
-        def quantize_wv(h, tag):
-            wv_codes[h] = sb.tile([P, E // 2], U32, name="wv_codes%d" % h, tag=tag, align_bytes=64)
-            wv_scale[h] = sb.tile([P, E // 2], U8, name="wv_scale%d" % h, align_bytes=64)
-            nc.vector.quantize_mx(
-                wv_codes[h][:].bitcast(FP8X4), wv_scale[h][:], wv_dealt[:, 2 * h : 2 * h + 2].rearrange("p s m j -> p (s m j)")
-            )
-
-        quantize_wv(0, "wv_codes0")
+        wv_codes = sb.tile([P, E], U32, name="wv_codes", align_bytes=64)
+        wv_scale = sb.tile([P, E], U8, name="wv_scale", align_bytes=64)
+        nc.vector.quantize_mx(wv_codes[:].bitcast(FP8X4), wv_scale[:], wv_dealt[:].rearrange("p s m j -> p (s m j)"))
         emb_codes = sb.tile([P, I], U32, name="emb_codes", tag="emb_codes", align_bytes=64)
         first_half, second_half, whole = slice(0, I // 2), slice(I // 2, I), slice(0, I)
         for slots in (first_half, second_half):
             nc.vector.tensor_copy(emb_codes[:, slots], words[:].bitcast(U32).indirect(offs_sb[:, list_cols(slots)]))
-        quantize_wv(1, "words")
 
         pages = [sb.tile([P, T], F32, name="page%d" % j, tag="page%d" % j, align_bytes=64) for j in range(PACK)]
         for j in range(PACK):
@@ -105,12 +97,12 @@ def tile_attend_headpage_proj_pl_kernel(tc, emb_words, emb_scales, wv, base, wo,
 
         pieces = [(0, first_half, "bank0"), (1, whole, "bank1"), (0, second_half, "back0"), (2, whole, "bank2"), (3, whole, "bank3")]
         for n, (j, slots, tag) in enumerate(pieces):
-            plane_cols = slice(P * (j % 2), P * (j % 2 + 1))
+            plane_cols = slice(P * j, P * (j + 1))
             width = slots.stop - slots.start
             v_sb = sb.tile([P, width], F32, name="v_sb%d" % n, align_bytes=64)
             v_ps = ps.tile([P, width], F32, name="v_ps%d" % n, tag=tag)
             nc.tensor.matmul_mx(
-                v_ps[:], lhsT=wv_codes[j // 2][:, plane_cols].bitcast(FP8X4), lhsT_scale=wv_scale[j // 2][:, plane_cols],
+                v_ps[:], lhsT=wv_codes[:, plane_cols].bitcast(FP8X4), lhsT_scale=wv_scale[:, plane_cols],
                 rhs=emb_codes[:, slots].bitcast(FP8X4), rhs_scale=emb_scale[:, slots], start=True, stop=True,
             )
             nc.scalar.copy(v_sb[:], v_ps[:])
@@ -202,11 +194,11 @@ def tile_attend_headpage_proj_pl_kernel(tc, emb_words, emb_scales, wv, base, wo,
             cols = chunk_cols(first, stop)
             nc.vector.quantize_mx(y_codes[:, cols].bitcast(FP8X4), y_scale[:, cols], y_woven[:, cols].rearrange("p t j -> p (t j)"))
 
-        for j in range(TURNED_PLANES, PACK):
-            for c in range(2):
-                add_base(j, c, c + 1)
-        for j in range(TURNED_PLANES, PACK):
-            add_base(j, 2, CHUNKS)
+        add_base(2, 0, 1)
+        add_base(3, 0, 1)
+        add_base(2, 1, CHUNKS)
+        add_base(3, 1, 2)
+        add_base(3, 2, CHUNKS)
         quantize_wo(0, "page2")
         for c in range(LAST):
             weave_x(c, nc.scalar.copy, "x_woven%d" % c)

@@ -1,7 +1,6 @@
 from contextlib import ExitStack
 
 import concourse.mybir as mybir
-from concourse.masks import make_identity
 
 K, U, I, T, E, F = 512, 2048, 256, 512, 512, 512
 FLOPS = 2 * K * E * I + 2 * E * F * T
@@ -14,6 +13,7 @@ U16 = mybir.dt.uint16
 U8 = mybir.dt.uint8
 FP8X4 = mybir.dt.float8_e4m3fn_x4
 ADD = mybir.AluOpType.add
+COPY = mybir.ActivationFunctionType.Copy
 
 P = 128
 PACK = 4
@@ -22,8 +22,8 @@ LIST_ROWS = 16
 CHUNK = 128
 CHUNKS = T // CHUNK
 LAST = CHUNKS - 1
-TURNED_PLANES = 2
 VECTOR_SHARE = 88
+VECTOR_PIECES = 2
 EARLY_CHUNKS = 2
 
 
@@ -77,7 +77,10 @@ def tile_attend_headpage_proj_pl_kernel(tc, emb_words, emb_scales, wv, base, wo,
 
         wv_dealt = sb.tile([P, PACK, P, PACK], BF16, name="wv_dealt", align_bytes=64)
         deal(nc.vector.tensor_copy, wv_dealt[:, :, :VECTOR_SHARE, :], wv_raw[:, :, : PACK * VECTOR_SHARE])
-        deal(nc.scalar.copy, wv_dealt[:, :, VECTOR_SHARE:, :], wv_raw[:, :, PACK * VECTOR_SHARE :])
+        scalar_dealt = wv_dealt[:, :, VECTOR_SHARE:, :].rearrange("p (a b) m j -> p a m j b", b=2)
+        scalar_raw = wv_raw[:, :, PACK * VECTOR_SHARE :].rearrange("p j (m a b) -> p a m j b", a=2, b=2)
+        for a in range(2):
+            nc.scalar.activation(scalar_dealt[:, a], scalar_raw[:, a], COPY)
         emb_scale = sb.tile([P, I], U8, name="emb_scale", align_bytes=64)
         nc.vector.tensor_copy(emb_scale[:], scale_rows[:].indirect(offs_sb[:]))
         wv_codes = sb.tile([P, E], U32, name="wv_codes", align_bytes=64)
@@ -92,26 +95,27 @@ def tile_attend_headpage_proj_pl_kernel(tc, emb_words, emb_scales, wv, base, wo,
         for j in range(PACK):
             nc.vector.memset(pages[j][:], 0.0)
 
-        ident = sb.tile([P, P], F32, name="ident", align_bytes=64)
-        make_identity(nc, ident[:])
-
-        pieces = [(0, first_half, "bank0"), (1, whole, "bank1"), (0, second_half, "back0"), (2, whole, "bank2"), (3, whole, "bank3")]
-        for n, (j, slots, tag) in enumerate(pieces):
+        pieces = [(3, first_half), (0, whole), (1, whole), (2, whole), (3, second_half)]
+        v_sb = []
+        for n, (j, slots) in enumerate(pieces):
             plane_cols = slice(P * j, P * (j + 1))
             width = slots.stop - slots.start
-            v_sb = sb.tile([P, width], F32, name="v_sb%d" % n, align_bytes=64)
-            v_ps = ps.tile([P, width], F32, name="v_ps%d" % n, tag=tag)
+            v_sb.append(sb.tile([P, width], F32, name="v_sb%d" % n, align_bytes=64))
+            v_ps = ps.tile([P, width], F32, name="v_ps%d" % n, tag="bank%d" % n)
             nc.tensor.matmul_mx(
                 v_ps[:], lhsT=wv_codes[:, plane_cols].bitcast(FP8X4), lhsT_scale=wv_scale[:, plane_cols],
                 rhs=emb_codes[:, slots].bitcast(FP8X4), rhs_scale=emb_scale[:, slots], start=True, stop=True,
             )
-            nc.scalar.copy(v_sb[:], v_ps[:])
-            nc.vector.tensor_copy(pages[j][:].indirect(offs2_sb[:, list_cols(slots)]), v_sb[:])
+            nc.scalar.copy(v_sb[n][:], v_ps[:])
+        for n, (j, slots) in enumerate(pieces):
+            places = pages[j][:].indirect(offs2_sb[:, list_cols(slots)])
+            if n < VECTOR_PIECES:
+                nc.vector.tensor_copy(places, v_sb[n][:])
+            else:
+                nc.scalar.activation(places, v_sb[n][:], COPY)
 
-        ident_bf = sb.tile([P, P], BF16, name="ident_bf", tag="emb_codes", align_bytes=64)
-        nc.scalar.copy(ident_bf[:], ident[:])
         wo_dealt = sb.tile([P, PACK, P, PACK], BF16, name="wo_dealt", align_bytes=64)
-        deal(nc.scalar.copy, wo_dealt[:], wo_raw[:])
+        deal(nc.vector.tensor_copy, wo_dealt[:], wo_raw[:])
 
         x_first = sb.tile([P, PACK, CHUNK], BF16, name="x_first", tag="x_first", align_bytes=64)
         x_rest = sb.tile([P, PACK, T - CHUNK], BF16, name="x_rest", align_bytes=64)
@@ -123,28 +127,6 @@ def tile_attend_headpage_proj_pl_kernel(tc, emb_words, emb_scales, wv, base, wo,
             cols = chunk_cols(first, stop)
             nc.vector.tensor_tensor(x_plane(j, first, stop), pages[j][:, cols], base_sb[j // 2][:, j % 2, cols], ADD)
 
-        turned = sb.tile([P, TURNED_PLANES, CHUNKS, P], BF16, name="turned", tag="wo_raw", align_bytes=64)
-        sums = [ps.tile([P, CHUNKS, P], F32, name="sum_ps%d" % j, tag="sum%d" % j) for j in range(TURNED_PLANES)]
-        for j in range(TURNED_PLANES):
-            for c in range(CHUNKS):
-                nc.tensor.matmul(
-                    sums[j][:, c, :], lhsT=base_sb[j // 2][:, j % 2, chunk_cols(c, c + 1)], rhs=ident[:],
-                    is_transpose=True, start=(c == 0), stop=False,
-                )
-        for j in (1, 0):
-            for c in range(CHUNKS):
-                nc.tensor.matmul(
-                    sums[j][:, c, :], lhsT=pages[j][:, chunk_cols(c, c + 1)], rhs=ident[:],
-                    is_transpose=True, start=False, stop=(c == LAST),
-                )
-            nc.scalar.copy(turned[:, j], sums[j][:])
-        for j in (1, 0):
-            back_ps = ps.tile([P, T], BF16, name="back_ps%d" % j, tag="back%d" % j)
-            for c in range(CHUNKS):
-                nc.tensor.transpose(back_ps[:, chunk_cols(c, c + 1)], turned[:, j, c, :], ident_bf[:])
-            nc.scalar.copy(x_plane(j, 0, 1), back_ps[:, chunk_cols(0, 1)])
-            nc.scalar.copy(x_plane(j, 1, CHUNKS), back_ps[:, chunk_cols(1, CHUNKS)])
-
         wo_codes = {}
         wo_scale = sb.tile([P, F], U8, name="wo_scale", align_bytes=64)
         y_sb = sb.tile([P, PACK, T], F32, name="y_sb", align_bytes=64)
@@ -154,7 +136,7 @@ def tile_attend_headpage_proj_pl_kernel(tc, emb_words, emb_scales, wv, base, wo,
         y_hbm = out_0.rearrange("(p s) t -> p s t", s=PACK)
         codes_hbm = out_1[0].rearrange("p t r -> p (t r)").bitcast(I32)
         x_woven, x_codes, x_scale, y_ps = {}, {}, {}, {}
-        y_banks = ["bank0", "bank1", "bank2", "bank3", "sum0", "sum1", "back0", "back1"]
+        y_banks = ["bank%d" % n for n in range(2 * CHUNKS)]
 
         def quantize_wo(h, reused_tag):
             wo_codes[h] = sb.tile([P, F // 2], U32, name="wo_codes%d" % h, tag=reused_tag, align_bytes=64)
@@ -194,6 +176,9 @@ def tile_attend_headpage_proj_pl_kernel(tc, emb_words, emb_scales, wv, base, wo,
             cols = chunk_cols(first, stop)
             nc.vector.quantize_mx(y_codes[:, cols].bitcast(FP8X4), y_scale[:, cols], y_woven[:, cols].rearrange("p t j -> p (t j)"))
 
+        for j in range(2):
+            add_base(j, 0, 1)
+            add_base(j, 1, CHUNKS)
         add_base(2, 0, 1)
         add_base(3, 0, 1)
         add_base(2, 1, CHUNKS)

@@ -19,6 +19,7 @@ P = 128
 PACK = 4
 QUADRANTS = 4
 LIST_ROWS = 16
+DMA_ALIGN = 256
 CHUNK = 128
 CHUNKS = T // CHUNK
 LAST = CHUNKS - 1
@@ -57,11 +58,11 @@ def tile_attend_headpage_proj_pl_kernel(tc, emb_words, emb_scales, wv, base, wo,
 
         offs_sb = sb.tile([P, I // LIST_ROWS], U16, name="offs_sb")
         offs2_sb = sb.tile([P, I // LIST_ROWS], U16, name="offs2_sb")
-        wv_raw = sb.tile([P, PACK, E], F32, name="wv_raw", align_bytes=64)
-        wo_raw = sb.tile([P, PACK, F], F32, name="wo_raw", tag="wo_raw", align_bytes=64)
-        base_sb = [sb.tile([P, 2, T], F32, name="base_sb%d" % h, align_bytes=64) for h in range(2)]
-        words = sb.tile([P, U], I32, name="words", tag="words", align_bytes=64)
-        scale_rows = sb.tile([P, U], U8, name="scale_rows", align_bytes=64)
+        wv_raw = sb.tile([P, PACK, E], F32, name="wv_raw", align_bytes=DMA_ALIGN)
+        wo_raw = sb.tile([P, PACK, F], F32, name="wo_raw", align_bytes=DMA_ALIGN)
+        base_sb = [sb.tile([P, 2, T], F32, name="base_sb%d" % h, align_bytes=DMA_ALIGN) for h in range(2)]
+        words = sb.tile([P, U], I32, name="words", align_bytes=DMA_ALIGN)
+        scale_rows = sb.tile([P, U], U8, name="scale_rows", align_bytes=DMA_ALIGN)
 
         nc.vector.memset(scale_rows[:].bitcast(I32), 0)
         nc.sync.dma_start(wv_raw[:], wv.rearrange("(p j) e -> p j e", j=PACK))
@@ -86,7 +87,7 @@ def tile_attend_headpage_proj_pl_kernel(tc, emb_words, emb_scales, wv, base, wo,
         wv_codes = sb.tile([P, E], U32, name="wv_codes", align_bytes=64)
         wv_scale = sb.tile([P, E], U8, name="wv_scale", align_bytes=64)
         nc.vector.quantize_mx(wv_codes[:].bitcast(FP8X4), wv_scale[:], wv_dealt[:].rearrange("p s m j -> p (s m j)"))
-        emb_codes = sb.tile([P, I], U32, name="emb_codes", tag="emb_codes", align_bytes=64)
+        emb_codes = sb.tile([P, I], U32, name="emb_codes", align_bytes=64)
         first_half, second_half, whole = slice(0, I // 2), slice(I // 2, I), slice(0, I)
         for slots in (first_half, second_half):
             nc.vector.tensor_copy(emb_codes[:, slots], words[:].bitcast(U32).indirect(offs_sb[:, list_cols(slots)]))
@@ -117,22 +118,18 @@ def tile_attend_headpage_proj_pl_kernel(tc, emb_words, emb_scales, wv, base, wo,
         wo_dealt = sb.tile([P, PACK, P, PACK], BF16, name="wo_dealt", align_bytes=64)
         deal(nc.vector.tensor_copy, wo_dealt[:], wo_raw[:])
 
-        x_first = sb.tile([P, PACK, CHUNK], BF16, name="x_first", tag="x_first", align_bytes=64)
-        x_rest = sb.tile([P, PACK, T - CHUNK], BF16, name="x_rest", align_bytes=64)
-
-        def x_plane(j, first, stop):
-            return x_first[:, j, :] if first == 0 else x_rest[:, j, chunk_cols(first - 1, stop - 1)]
+        x_planes = sb.tile([P, PACK, T], BF16, name="x_planes", align_bytes=64)
 
         def add_base(j, first, stop):
             cols = chunk_cols(first, stop)
-            nc.vector.tensor_tensor(x_plane(j, first, stop), pages[j][:, cols], base_sb[j // 2][:, j % 2, cols], ADD)
+            nc.vector.tensor_tensor(x_planes[:, j, cols], pages[j][:, cols], base_sb[j // 2][:, j % 2, cols], ADD)
 
         wo_codes = {}
         wo_scale = sb.tile([P, F], U8, name="wo_scale", align_bytes=64)
-        y_sb = sb.tile([P, PACK, T], F32, name="y_sb", align_bytes=64)
+        y_sb = sb.tile([P, PACK, T], F32, name="y_sb", align_bytes=DMA_ALIGN)
         y_woven = sb.tile([P, T, PACK], BF16, name="y_woven", align_bytes=64)
-        y_codes = sb.tile([P, T], U32, name="y_codes", align_bytes=64)
-        y_scale = sb.tile([P, T], U8, name="y_scale", align_bytes=64)
+        y_codes = sb.tile([P, T], U32, name="y_codes", align_bytes=DMA_ALIGN)
+        y_scale = sb.tile([P, T], U8, name="y_scale", align_bytes=DMA_ALIGN)
         y_hbm = out_0.rearrange("(p s) t -> p s t", s=PACK)
         codes_hbm = out_1[0].rearrange("p t r -> p (t r)").bitcast(I32)
         x_woven, x_codes, x_scale, y_ps = {}, {}, {}, {}
@@ -147,7 +144,7 @@ def tile_attend_headpage_proj_pl_kernel(tc, emb_words, emb_scales, wv, base, wo,
 
         def weave_x(c, engine_copy, tag):
             x_woven[c] = sb.tile([P, CHUNK, PACK], BF16, name="x_woven%d" % c, tag=tag, align_bytes=64)
-            weave(engine_copy, x_woven[c][:], x_plane(slice(0, PACK), c, c + 1))
+            weave(engine_copy, x_woven[c][:], x_planes[:, :, chunk_cols(c, c + 1)])
 
         def quantize_x(c):
             x_codes[c] = sb.tile([P, CHUNK], U32, name="x_codes%d" % c, align_bytes=64)
@@ -176,19 +173,18 @@ def tile_attend_headpage_proj_pl_kernel(tc, emb_words, emb_scales, wv, base, wo,
             cols = chunk_cols(first, stop)
             nc.vector.quantize_mx(y_codes[:, cols].bitcast(FP8X4), y_scale[:, cols], y_woven[:, cols].rearrange("p t j -> p (t j)"))
 
-        for j in range(2):
-            add_base(j, 0, 1)
-            add_base(j, 1, CHUNKS)
+        add_base(0, 0, CHUNKS)
+        add_base(1, 0, CHUNKS)
         add_base(2, 0, 1)
         add_base(3, 0, 1)
         add_base(2, 1, CHUNKS)
         add_base(3, 1, 2)
-        add_base(3, 2, CHUNKS)
         quantize_wo(0, "page2")
+        add_base(3, 2, CHUNKS)
         for c in range(LAST):
             weave_x(c, nc.scalar.copy, "x_woven%d" % c)
         quantize_x(0)
-        quantize_wo(1, "x_first")
+        quantize_wo(1, "page3")
         quantize_x(1)
         quantize_x(2)
         weave_x(LAST, nc.vector.tensor_copy, "x_woven1")

@@ -25,6 +25,7 @@ CHUNKS = T // CHUNK
 LAST = CHUNKS - 1
 VECTOR_SHARE = 88
 VECTOR_PIECES = 2
+WO_SHARE = 96
 EARLY_CHUNKS = 2
 
 
@@ -116,7 +117,8 @@ def tile_attend_headpage_proj_pl_kernel(tc, emb_words, emb_scales, wv, base, wo,
                 nc.scalar.activation(places, v_sb[n][:], COPY)
 
         wo_dealt = sb.tile([P, PACK, P, PACK], BF16, name="wo_dealt", align_bytes=64)
-        deal(nc.vector.tensor_copy, wo_dealt[:], wo_raw[:])
+        deal(nc.vector.tensor_copy, wo_dealt[:, :, :WO_SHARE, :], wo_raw[:, :, : PACK * WO_SHARE])
+        deal(nc.scalar.copy, wo_dealt[:, :, WO_SHARE:, :], wo_raw[:, :, PACK * WO_SHARE :])
 
         x_planes = sb.tile([P, PACK, T], BF16, name="x_planes", align_bytes=64)
 

@@ -88,7 +88,7 @@ def tile_attend_headpage_proj_pl_kernel(tc, emb_words, emb_scales, wv, base, wo,
         wv_codes = sb.tile([P, E], U32, name="wv_codes", align_bytes=64)
         wv_scale = sb.tile([P, E], U8, name="wv_scale", align_bytes=64)
         nc.vector.quantize_mx(wv_codes[:].bitcast(FP8X4), wv_scale[:], wv_dealt[:].rearrange("p s m j -> p (s m j)"))
-        emb_codes = sb.tile([P, I], U32, name="emb_codes", align_bytes=64)
+        emb_codes = sb.tile([P, I], U32, name="emb_codes", tag="emb_codes", align_bytes=64)
         first_half, second_half, whole = slice(0, I // 2), slice(I // 2, I), slice(0, I)
         for slots in (first_half, second_half):
             nc.vector.tensor_copy(emb_codes[:, slots], words[:].bitcast(U32).indirect(offs_sb[:, list_cols(slots)]))
@@ -108,7 +108,7 @@ def tile_attend_headpage_proj_pl_kernel(tc, emb_words, emb_scales, wv, base, wo,
                 v_ps[:], lhsT=wv_codes[:, plane_cols].bitcast(FP8X4), lhsT_scale=wv_scale[:, plane_cols],
                 rhs=emb_codes[:, slots].bitcast(FP8X4), rhs_scale=emb_scale[:, slots], start=True, stop=True,
             )
-            nc.scalar.copy(v_sb[n][:], v_ps[:])
+            (nc.vector.tensor_copy if n == len(pieces) - 1 else nc.scalar.copy)(v_sb[n][:], v_ps[:])
         for n, (j, slots) in enumerate(pieces):
             places = pages[j][:].indirect(offs2_sb[:, list_cols(slots)])
             if n < VECTOR_PIECES:
@@ -116,7 +116,7 @@ def tile_attend_headpage_proj_pl_kernel(tc, emb_words, emb_scales, wv, base, wo,
             else:
                 nc.scalar.activation(places, v_sb[n][:], COPY)
 
-        wo_dealt = sb.tile([P, PACK, P, PACK], BF16, name="wo_dealt", align_bytes=64)
+        wo_dealt = sb.tile([P, PACK, P, PACK], BF16, name="wo_dealt", tag="emb_codes", align_bytes=64)
         deal(nc.vector.tensor_copy, wo_dealt[:, :, :WO_SHARE, :], wo_raw[:, :, : PACK * WO_SHARE])
         deal(nc.scalar.copy, wo_dealt[:, :, WO_SHARE:, :], wo_raw[:, :, PACK * WO_SHARE :])
 

@@ -24,8 +24,9 @@ CHUNK = 128
 CHUNKS = T // CHUNK
 LAST = CHUNKS - 1
 VECTOR_SHARE = 88
-VECTOR_PIECES = 2
-WO_SHARE = 96
+VECTOR_PIECES = (0, 3)
+WO_SHARE = 88
+SCALAR_PLANES = (1, 2)
 EARLY_CHUNKS = 2
 
 
@@ -95,9 +96,9 @@ def tile_attend_headpage_proj_pl_kernel(tc, emb_words, emb_scales, wv, base, wo,
 
         pages = [sb.tile([P, T], F32, name="page%d" % j, tag="page%d" % j, align_bytes=64) for j in range(PACK)]
         for j in range(PACK):
-            nc.vector.memset(pages[j][:], 0.0)
+            (nc.gpsimd if j in SCALAR_PLANES else nc.vector).memset(pages[j][:], 0.0)
 
-        pieces = [(3, first_half), (0, whole), (1, whole), (2, whole), (3, second_half)]
+        pieces = [(3, first_half), (1, whole), (2, whole), (0, whole), (3, second_half)]
         v_sb = []
         for n, (j, slots) in enumerate(pieces):
             plane_cols = slice(P * j, P * (j + 1))
@@ -108,10 +109,10 @@ def tile_attend_headpage_proj_pl_kernel(tc, emb_words, emb_scales, wv, base, wo,
                 v_ps[:], lhsT=wv_codes[:, plane_cols].bitcast(FP8X4), lhsT_scale=wv_scale[:, plane_cols],
                 rhs=emb_codes[:, slots].bitcast(FP8X4), rhs_scale=emb_scale[:, slots], start=True, stop=True,
             )
-            (nc.vector.tensor_copy if n == len(pieces) - 1 else nc.scalar.copy)(v_sb[n][:], v_ps[:])
+            (nc.vector.tensor_copy if n >= 3 else nc.scalar.copy)(v_sb[n][:], v_ps[:])
         for n, (j, slots) in enumerate(pieces):
             places = pages[j][:].indirect(offs2_sb[:, list_cols(slots)])
-            if n < VECTOR_PIECES:
+            if n in VECTOR_PIECES:
                 nc.vector.tensor_copy(places, v_sb[n][:])
             else:
                 nc.scalar.activation(places, v_sb[n][:], COPY)

@@ -24,9 +24,7 @@ CHUNK = 128
 CHUNKS = T // CHUNK
 LAST = CHUNKS - 1
 VECTOR_SHARE = 88
-VECTOR_PIECES = (0, 3)
-WO_SHARE = 88
-SCALAR_PLANES = (1, 2)
+WO_SHARE = 76
 EARLY_CHUNKS = 2
 
 
@@ -95,27 +93,35 @@ def tile_attend_headpage_proj_pl_kernel(tc, emb_words, emb_scales, wv, base, wo,
             nc.vector.tensor_copy(emb_codes[:, slots], words[:].bitcast(U32).indirect(offs_sb[:, list_cols(slots)]))
 
         pages = [sb.tile([P, T], F32, name="page%d" % j, tag="page%d" % j, align_bytes=64) for j in range(PACK)]
-        for j in range(PACK):
-            (nc.gpsimd if j in SCALAR_PLANES else nc.vector).memset(pages[j][:], 0.0)
+        for j in (0, 2, 1, 3):
+            nc.gpsimd.memset(pages[j][:], 0.0)
 
-        pieces = [(3, first_half), (1, whole), (2, whole), (0, whole), (3, second_half)]
-        v_sb = []
+        pieces = [(3, first_half), (1, first_half), (1, second_half), (2, whole), (0, whole), (3, second_half)]
+        banks, v_sb = [], []
         for n, (j, slots) in enumerate(pieces):
             plane_cols = slice(P * j, P * (j + 1))
             width = slots.stop - slots.start
             v_sb.append(sb.tile([P, width], F32, name="v_sb%d" % n, align_bytes=64))
-            v_ps = ps.tile([P, width], F32, name="v_ps%d" % n, tag="bank%d" % n)
+            banks.append(ps.tile([P, width], F32, name="v_ps%d" % n, tag="bank%d" % n))
             nc.tensor.matmul_mx(
-                v_ps[:], lhsT=wv_codes[:, plane_cols].bitcast(FP8X4), lhsT_scale=wv_scale[:, plane_cols],
+                banks[n][:], lhsT=wv_codes[:, plane_cols].bitcast(FP8X4), lhsT_scale=wv_scale[:, plane_cols],
                 rhs=emb_codes[:, slots].bitcast(FP8X4), rhs_scale=emb_scale[:, slots], start=True, stop=True,
             )
-            (nc.vector.tensor_copy if n >= 3 else nc.scalar.copy)(v_sb[n][:], v_ps[:])
-        for n, (j, slots) in enumerate(pieces):
-            places = pages[j][:].indirect(offs2_sb[:, list_cols(slots)])
-            if n in VECTOR_PIECES:
-                nc.vector.tensor_copy(places, v_sb[n][:])
-            else:
-                nc.scalar.activation(places, v_sb[n][:], COPY)
+
+        def places(n):
+            j, slots = pieces[n]
+            return pages[j][:].indirect(offs2_sb[:, list_cols(slots)])
+
+        for n in range(3):
+            nc.scalar.copy(v_sb[n][:], banks[n][:])
+        nc.vector.tensor_copy(places(0), v_sb[0][:])
+        nc.scalar.activation(places(1), v_sb[1][:], COPY)
+        nc.scalar.copy(v_sb[3][:], banks[3][:])
+        for n in (4, 5):
+            nc.vector.tensor_copy(v_sb[n][:], banks[n][:])
+        nc.vector.tensor_copy(places(4), v_sb[4][:])
+        for n in (2, 3, 5):
+            nc.scalar.activation(places(n), v_sb[n][:], COPY)
 
         wo_dealt = sb.tile([P, PACK, P, PACK], BF16, name="wo_dealt", tag="emb_codes", align_bytes=64)
         deal(nc.vector.tensor_copy, wo_dealt[:, :, :WO_SHARE, :], wo_raw[:, :, : PACK * WO_SHARE])

@@ -25,6 +25,7 @@ CHUNKS = T // CHUNK
 LAST = CHUNKS - 1
 VECTOR_SHARE = 88
 WO_SHARE = 76
+GPSIMD_PAGE = 2
 EARLY_CHUNKS = 2
 
 
@@ -93,8 +94,8 @@ def tile_attend_headpage_proj_pl_kernel(tc, emb_words, emb_scales, wv, base, wo,
             nc.vector.tensor_copy(emb_codes[:, slots], words[:].bitcast(U32).indirect(offs_sb[:, list_cols(slots)]))
 
         pages = [sb.tile([P, T], F32, name="page%d" % j, tag="page%d" % j, align_bytes=64) for j in range(PACK)]
-        for j in (0, 2, 1, 3):
-            nc.gpsimd.memset(pages[j][:], 0.0)
+        for j in range(PACK):
+            (nc.gpsimd if j == GPSIMD_PAGE else nc.vector).memset(pages[j][:], 0.0)
 
         pieces = [(3, first_half), (1, first_half), (1, second_half), (2, whole), (0, whole), (3, second_half)]
         banks, v_sb = [], []

from contextlib import ExitStack

import concourse.mybir as mybir

K, U, I, T, E, F = 512, 2048, 256, 512, 512, 512
FLOPS = 2 * K * E * I + 2 * E * F * T

F32 = mybir.dt.float32
BF16 = mybir.dt.bfloat16
I32 = mybir.dt.int32
U32 = mybir.dt.uint32
U16 = mybir.dt.uint16
U8 = mybir.dt.uint8
FP8X4 = mybir.dt.float8_e4m3fn_x4
ADD = mybir.AluOpType.add
COPY = mybir.ActivationFunctionType.Copy

P = 128
PACK = 4
QUADRANTS = 4
LIST_ROWS = 16
DMA_ALIGN = 256
CHUNK = 128
CHUNKS = T // CHUNK
LAST = CHUNKS - 1
VECTOR_SHARE = 88
WO_SHARE = 76
GPSIMD_PAGE = 2
EARLY_CHUNKS = 2


def deal(engine_copy, dealt, raw):
    engine_copy(
        dealt.rearrange("p (a b) m j -> p a m j b", b=2),
        raw.rearrange("p j (m a b) -> p a m j b", a=2, b=2),
    )


def weave(engine_copy, woven, planes):
    engine_copy(
        woven.rearrange("p (c i) j -> p c j i", i=4),
        planes.rearrange("p j (c i) -> p c j i", i=4),
    )


def chunk_cols(first, stop):
    return slice(CHUNK * first, CHUNK * stop)


def list_cols(slots):
    return slice(slots.start // LIST_ROWS, slots.stop // LIST_ROWS)


def tile_attend_headpage_proj_pl_kernel(tc, emb_words, emb_scales, wv, base, wo, offs, offs2, out_0, out_1, out_2):
    nc = tc.nc
    with ExitStack() as ctx:
        sb = ctx.enter_context(tc.tile_pool(name="sb", bufs=1))
        ps = ctx.enter_context(tc.psum_pool(name="ps", bufs=1))

        offs_sb = sb.tile([P, I // LIST_ROWS], U16, name="offs_sb")
        offs2_sb = sb.tile([P, I // LIST_ROWS], U16, name="offs2_sb")
        wv_raw = sb.tile([P, PACK, E], F32, name="wv_raw", align_bytes=DMA_ALIGN)
        wo_raw = sb.tile([P, PACK, F], F32, name="wo_raw", align_bytes=DMA_ALIGN)
        base_sb = [sb.tile([P, 2, T], F32, name="base_sb%d" % h, align_bytes=DMA_ALIGN) for h in range(2)]
        words = sb.tile([P, U], I32, name="words", align_bytes=DMA_ALIGN)
        scale_rows = sb.tile([P, U], U8, name="scale_rows", align_bytes=DMA_ALIGN)

        nc.vector.memset(scale_rows[:].bitcast(I32), 0)
        nc.sync.dma_start(wv_raw[:], wv.rearrange("(p j) e -> p j e", j=PACK))
        for r in range(PACK):
            nc.sync.dma_start(scale_rows[r:P:32, :].bitcast(I32), emb_scales[0, r : 16 : PACK, :].bitcast(I32))
        nc.sync.dma_start(offs_sb[:], offs)
        nc.sync.dma_start(words[:], emb_words[0].rearrange("p u r -> p (u r)").bitcast(I32))
        nc.sync.dma_start(offs2_sb[:], offs2)
        base_hbm = base.rearrange("(p j) t -> p j t", j=PACK)
        nc.sync.dma_start(wo_raw[:], wo.rearrange("(p j) f -> p j f", j=PACK))
        nc.sync.dma_start(base_sb[0][:], base_hbm[:, 0:2, :])
        nc.sync.dma_start(base_sb[1][:], base_hbm[:, 2:4, :])

        wv_dealt = sb.tile([P, PACK, P, PACK], BF16, name="wv_dealt", align_bytes=64)
        deal(nc.vector.tensor_copy, wv_dealt[:, :, :VECTOR_SHARE, :], wv_raw[:, :, : PACK * VECTOR_SHARE])
        scalar_dealt = wv_dealt[:, :, VECTOR_SHARE:, :].rearrange("p (a b) m j -> p a m j b", b=2)
        scalar_raw = wv_raw[:, :, PACK * VECTOR_SHARE :].rearrange("p j (m a b) -> p a m j b", a=2, b=2)
        for a in range(2):
            nc.scalar.activation(scalar_dealt[:, a], scalar_raw[:, a], COPY)
        emb_scale = sb.tile([P, I], U8, name="emb_scale", align_bytes=64)
        nc.vector.tensor_copy(emb_scale[:], scale_rows[:].indirect(offs_sb[:]))
        wv_codes = sb.tile([P, E], U32, name="wv_codes", align_bytes=64)
        wv_scale = sb.tile([P, E], U8, name="wv_scale", align_bytes=64)
        nc.vector.quantize_mx(wv_codes[:].bitcast(FP8X4), wv_scale[:], wv_dealt[:].rearrange("p s m j -> p (s m j)"))
        emb_codes = sb.tile([P, I], U32, name="emb_codes", tag="emb_codes", align_bytes=64)
        first_half, second_half, whole = slice(0, I // 2), slice(I // 2, I), slice(0, I)
        for slots in (first_half, second_half):
            nc.vector.tensor_copy(emb_codes[:, slots], words[:].bitcast(U32).indirect(offs_sb[:, list_cols(slots)]))

        pages = [sb.tile([P, T], F32, name="page%d" % j, tag="page%d" % j, align_bytes=64) for j in range(PACK)]
        for j in range(PACK):
            (nc.gpsimd if j == GPSIMD_PAGE else nc.vector).memset(pages[j][:], 0.0)

        pieces = [(3, first_half), (1, first_half), (1, second_half), (2, whole), (0, whole), (3, second_half)]
        banks, v_sb = [], []
        for n, (j, slots) in enumerate(pieces):
            plane_cols = slice(P * j, P * (j + 1))
            width = slots.stop - slots.start
            v_sb.append(sb.tile([P, width], F32, name="v_sb%d" % n, align_bytes=64))
            banks.append(ps.tile([P, width], F32, name="v_ps%d" % n, tag="bank%d" % n))
            nc.tensor.matmul_mx(
                banks[n][:], lhsT=wv_codes[:, plane_cols].bitcast(FP8X4), lhsT_scale=wv_scale[:, plane_cols],
                rhs=emb_codes[:, slots].bitcast(FP8X4), rhs_scale=emb_scale[:, slots], start=True, stop=True,
            )

        def places(n):
            j, slots = pieces[n]
            return pages[j][:].indirect(offs2_sb[:, list_cols(slots)])

        for n in range(3):
            nc.scalar.copy(v_sb[n][:], banks[n][:])
        nc.vector.tensor_copy(places(0), v_sb[0][:])
        nc.scalar.activation(places(1), v_sb[1][:], COPY)
        nc.scalar.copy(v_sb[3][:], banks[3][:])
        for n in (4, 5):
            nc.vector.tensor_copy(v_sb[n][:], banks[n][:])
        nc.vector.tensor_copy(places(4), v_sb[4][:])
        for n in (2, 3, 5):
            nc.scalar.activation(places(n), v_sb[n][:], COPY)

        wo_dealt = sb.tile([P, PACK, P, PACK], BF16, name="wo_dealt", tag="emb_codes", align_bytes=64)
        deal(nc.vector.tensor_copy, wo_dealt[:, :, :WO_SHARE, :], wo_raw[:, :, : PACK * WO_SHARE])
        deal(nc.scalar.copy, wo_dealt[:, :, WO_SHARE:, :], wo_raw[:, :, PACK * WO_SHARE :])

        x_planes = sb.tile([P, PACK, T], BF16, name="x_planes", align_bytes=64)

        def add_base(j, first, stop):
            cols = chunk_cols(first, stop)
            nc.vector.tensor_tensor(x_planes[:, j, cols], pages[j][:, cols], base_sb[j // 2][:, j % 2, cols], ADD)

        wo_codes = {}
        wo_scale = sb.tile([P, F], U8, name="wo_scale", align_bytes=64)
        y_sb = sb.tile([P, PACK, T], F32, name="y_sb", align_bytes=DMA_ALIGN)
        y_woven = sb.tile([P, T, PACK], BF16, name="y_woven", align_bytes=64)
        y_codes = sb.tile([P, T], U32, name="y_codes", align_bytes=DMA_ALIGN)
        y_scale = sb.tile([P, T], U8, name="y_scale", align_bytes=DMA_ALIGN)
        y_hbm = out_0.rearrange("(p s) t -> p s t", s=PACK)
        codes_hbm = out_1[0].rearrange("p t r -> p (t r)").bitcast(I32)
        x_woven, x_codes, x_scale, y_ps = {}, {}, {}, {}
        y_banks = ["bank%d" % n for n in range(2 * CHUNKS)]

        def quantize_wo(h, reused_tag):
            wo_codes[h] = sb.tile([P, F // 2], U32, name="wo_codes%d" % h, tag=reused_tag, align_bytes=64)
            nc.vector.quantize_mx(
                wo_codes[h][:].bitcast(FP8X4), wo_scale[:, F // 2 * h : F // 2 * (h + 1)],
                wo_dealt[:, 2 * h : 2 * h + 2].rearrange("p s m j -> p (s m j)"),
            )

        def weave_x(c, engine_copy, tag):
            x_woven[c] = sb.tile([P, CHUNK, PACK], BF16, name="x_woven%d" % c, tag=tag, align_bytes=64)
            weave(engine_copy, x_woven[c][:], x_planes[:, :, chunk_cols(c, c + 1)])

        def quantize_x(c):
            x_codes[c] = sb.tile([P, CHUNK], U32, name="x_codes%d" % c, align_bytes=64)
            x_scale[c] = sb.tile([P, CHUNK], U8, name="x_scale%d" % c, align_bytes=64)
            nc.vector.quantize_mx(x_codes[c][:].bitcast(FP8X4), x_scale[c][:], x_woven[c][:].rearrange("p t j -> p (t j)"))

        def project(c):
            for s in range(PACK):
                if s % 2 == 0:
                    y_ps[c, s // 2] = ps.tile([P, 2, CHUNK], F32, name="y_ps%d_%d" % (c, s // 2), tag=y_banks[2 * c + s // 2])
                nc.tensor.matmul_mx(
                    y_ps[c, s // 2][:, s % 2, :],
                    lhsT=wo_codes[s // 2][:, P * (s % 2) : P * (s % 2 + 1)].bitcast(FP8X4),
                    lhsT_scale=wo_scale[:, P * s : P * (s + 1)],
                    rhs=x_codes[c][:].bitcast(FP8X4), rhs_scale=x_scale[c][:], start=True, stop=True,
                )

        def hand_out(c):
            cols = chunk_cols(c, c + 1)
            for h in range(2):
                nc.scalar.copy(y_sb[:, 2 * h : 2 * h + 2, cols], y_ps[c, h][:])
            nc.sync.dma_start(y_hbm[:, :, cols], y_sb[:, :, cols])
            weave(nc.vector.tensor_copy, y_woven[:, cols], y_sb[:, :, cols])

        def quantize_y(first, stop):
            cols = chunk_cols(first, stop)
            nc.vector.quantize_mx(y_codes[:, cols].bitcast(FP8X4), y_scale[:, cols], y_woven[:, cols].rearrange("p t j -> p (t j)"))

        add_base(0, 0, CHUNKS)
        add_base(1, 0, CHUNKS)
        add_base(2, 0, 1)
        add_base(3, 0, 1)
        add_base(2, 1, CHUNKS)
        add_base(3, 1, 2)
        quantize_wo(0, "page2")
        add_base(3, 2, CHUNKS)
        for c in range(LAST):
            weave_x(c, nc.scalar.copy, "x_woven%d" % c)
        quantize_x(0)
        quantize_wo(1, "page3")
        quantize_x(1)
        quantize_x(2)
        weave_x(LAST, nc.vector.tensor_copy, "x_woven1")
        quantize_x(LAST)
        for c in range(CHUNKS):
            project(c)

        for c in range(EARLY_CHUNKS):
            hand_out(c)
        quantize_y(0, EARLY_CHUNKS)
        early, late = chunk_cols(0, EARLY_CHUNKS), chunk_cols(EARLY_CHUNKS, CHUNKS)
        nc.sync.dma_start(codes_hbm[:, early], y_codes[:, early].bitcast(I32))
        for c in range(EARLY_CHUNKS, CHUNKS):
            hand_out(c)
        for c in range(EARLY_CHUNKS, CHUNKS):
            quantize_y(c, c + 1)
        nc.scalar.dma_start(codes_hbm[:, late], y_codes[:, late].bitcast(I32))
        for q in range(QUADRANTS):
            queue = nc.scalar if q % 2 else nc.sync
            queue.dma_start(out_2[0, 4 * q : 4 * q + 4, :].bitcast(I32), y_scale[32 * q : 32 * q + 4, :].bitcast(I32))
